import numpy as np, ml_dtypes
CORES = [25,29,65,69,153,157,193,197]
N = 8
import mx_ref
BF = ml_dtypes.bfloat16
def gentries(a):
    return np.ascontiguousarray(a.reshape(8, 16, -1).transpose(0, 2, 1)).reshape(8, -1)
def gtable(e):
    e = np.asarray(e); return np.ascontiguousarray(e.reshape(8, -1, 16).transpose(0, 2, 1)).reshape(128, -1).astype(np.int32)
def gcols(t, e):
    v = np.concatenate([t.reshape(8, 16, -1, 4), np.zeros((8, 16, 1, 4), BF)], axis=2)
    return np.ascontiguousarray(np.stack([v[g][:, e[g]] for g in range(8)])).reshape(128, -1)
def tile(rs):
    return np.stack(rs, axis=2).reshape(128, -1).astype(BF)
def pick(q, e):
    c = np.concatenate([q[0].reshape(128, -1, 4), np.zeros((128, 1, 4), np.uint8)], axis=1); s = np.concatenate([q[1], np.ones((16, 1), np.uint8)], axis=1)
    return (np.ascontiguousarray(c[:, e].reshape(128, -1)), np.ascontiguousarray(s[:, e]))
def join(*qs):
    return (np.concatenate([q[0] for q in qs], axis=1), np.concatenate([q[1] for q in qs], axis=1))
def put(q, e, v):
    c, s = q[0].reshape(128, -1, 4).copy(), q[1].copy(); c[:, e] = v[0].reshape(128, -1, 4); s[:, e] = v[1]
    return (c.reshape(128, -1), s)
def pk(c, s):
    return (np.ascontiguousarray(c), mx_ref.live(s))
def emit(q):
    return q[0], q[1]
def packed(v, rng):
    q = [mx_ref.quantize(np.ascontiguousarray(v[r])) for r in range(N)]
    return np.stack([a for a, b in q]), np.stack([mx_ref.plane(b, rng) for a, b in q])
def values_of_codes():
    e, c = np.zeros((128, 128, 4), np.float32), np.zeros((128, 2, 4), np.uint8)
    e[np.arange(128), np.arange(128), 0] = 1
    c[:127, :, 0] = np.arange(256).reshape(2, 128).T[:127]
    return mx_ref.matmul(mx_ref.quantize(e.reshape(128, 512).astype(BF)), (c.reshape(128, 8), np.full((16, 2), 127, np.uint8))).T.reshape(-1).astype(np.float64)
CODE_VALUE, SCALE_VALUE = values_of_codes(), 2.0 ** (np.arange(256) - 127.0)
def decode(q):
    return (CODE_VALUE[q[0]].reshape(16, 8, -1, 4) * SCALE_VALUE[q[1]][:, None, :, None] + 0.0).reshape(128, -1).astype(np.float32)
def f(rng, *shape):
    return mx_ref.flush((rng.standard_normal(shape, dtype=np.float32) * np.exp2(rng.integers(-2, 3, shape[:-1] + (1,)))).astype(BF))
def wide(rng, *shape, cols=0):
    v = rng.standard_normal(shape, dtype=np.float32) * np.exp2(rng.integers(-12, 13, shape)).astype(np.float32)
    if cols: v *= np.repeat(np.exp2(rng.integers(-cols, cols + 1, shape[:-2] + (1, shape[-1] // 4))) * (rng.random(shape[:-2] + (1, shape[-1] // 4)) > 0.0625), 4, axis=-1).astype(np.float32)
    return mx_ref.flush(v.astype(BF))
C = 288
STEP = [4, 1, 2]
HOPS = 128
def numbers_of(rng):
    return {"x": np.array(f(rng, N, 128, 4 * C)), "u": np.array(f(rng, N, 128, 512)), "v": np.array(f(rng, N, 128, 512))}
def orders(rng):
    e = np.tile(np.arange(C), (N, 8, 1))
    k, a, t = rng.permuted(e, axis=2), rng.permuted(e, axis=2)[:, :, 16:], e.copy()
    np.put_along_axis(t, a[:, :, 0::2], a[:, :, 1::2], axis=2)
    np.put_along_axis(t, a[:, :, 1::2], a[:, :, 0::2], axis=2)
    return k, t
def stored(k, t):
    return {"nx": np.stack([gtable(k[r]) for r in range(N)]), "mt": np.stack([gtable(t[r]) for r in range(N)])}
def layers(rng, still=[]):
    w = np.array(f(rng, N, 128, 2048)).reshape(N, 8, 16, 4, 8, 16, 4)
    for i in still:
        w[:, :, i] = 0
        w[:, :, :, :, :, i] = 0
    return w
def weights(rng, w):
    c, p = packed(np.ascontiguousarray(w).reshape(N, 128, 2048), rng)
    return {"wc": c, "ws": p}
def setup_inputs(rng):
    return {**numbers_of(rng), **stored(*orders(rng)), **weights(rng, layers(rng))}
def setup_inputs_ties(rng):
    d = numbers_of(rng)
    k, t = orders(rng)
    o = rng.permutation(N) % 4
    n = rng.integers(0, 4, (N, 8, C))
    c = np.ones((N, 8), np.float32)
    for r in range(N):
        c[r] = rng.permutation(8) % 2 * 2.0 - 1.0
        for g in range(8):
            if o[r] < 2:
                e = rng.permutation(C)
                a = np.arange(C) + 1 if c[r, g] < 0 else C - np.arange(C)
                n[r, g, e] = a if o[r] == 0 else (a + 1) // 2
                k[r, g, e] = np.roll(e, -1)
            if o[r] == 3: n[r, g] = rng.integers(0, 2, C) if g % 2 else 1
        if o[r] < 2: t[r, rng.permutation(8)[:4]] = np.arange(C)
    digits = (n[..., None] & (1 << np.arange(12))).reshape(N, 8, C, 3, 4)
    x = d["x"].reshape(N, 8, 16, C, 4)
    x[:, :, 8:] = 0
    x[:, :, 8:11] = digits.transpose(0, 1, 3, 2, 4).astype(np.float32).astype(BF)
    u = d["u"].reshape(N, 128, 128, 4)
    u[:, :, ::16] = 0
    for g in range(8): u[:, 16 * g + 8:16 * g + 11, 16 * g] = c[:, g].astype(BF)[:, None, None]
    w = layers(rng)
    w[:, :, :, :, :, 8:] = 0
    return {"x": x.reshape(N, 128, 4 * C), "u": u.reshape(N, 128, 512), "v": d["v"], **stored(k, t), **weights(rng, w)}
def setup_inputs_near(rng):
    d = numbers_of(rng)
    x = d["x"].astype(np.float32).reshape(N, 8, 16, C, 4)
    x[:, :, :2] = 0
    x[:, :, 8:] = 0
    u = d["u"].reshape(N, 128, 128, 4)
    u[:, :, ::16] = 0
    w = layers(rng, [0, 1, 8, 9, 10, 11, 12, 13, 14, 15])
    o = (np.arange(N) + rng.integers(N)) % 4
    for r in range(N):
        c = rng.choice([-1.0, 1.0], (8, 1))
        s = rng.integers(0, 16, (8, C))
        digits = ((s[:, :, None] >> np.arange(4)) & 1) * np.exp2(np.arange(4) - 23.0)
        if o[r] < 2:
            x[r, :, 0, :, 0] = c
            x[r, :, 8] = digits
            x[r, :, 11, :, 0] = 2.0 ** -10
        else:
            x[r, :, :8] = 0
            x[r, :, 13, :, 0] = 2.0 ** -30
            x[r, :, 1, :, 0] = rng.choice([-1.0, 1.0], (8, C)) * 2.0 ** -30
            w[r] = 0
            for g in range(8): w[r, g, 1, 0, g, 12, 0] = 2.0 ** -8
        if o[r] == 2: x[r, :, 8] = digits * rng.choice([-1.0, 1.0], (8, C, 1))
        if o[r] == 3:
            x[r, :, 8, :, 0] = np.where(s < 8, 1.25, 0.0) * 2.0 ** -30 * c
            x[r, :, 9, :, 0] = np.where(s < 8, 0.0, 1.125) * 2.0 ** -30 * c
            for g in rng.permutation(8)[:4]:
                e = rng.choice([-1.0, 1.0], C) * 2.0 ** -30
                x[r, g, 8, :, 0] = 1.25 * e
                x[r, g, 9, :, 0] = -1.125 * e
        at = [0, C - 1, int(rng.integers(C)), int(rng.integers(C))]
        for g, j in zip(rng.permutation(8)[:4], at): x[r, g, 0, j, 0] = 2.0 ** 29 * rng.choice([-1.0, 1.0])
        k = 1.0 if o[r] == 0 else 2.0 ** -30
        for h in range(0, 128, 16):
            u[r, h, h, 0] = k if o[r] < 2 else 1.0
            if o[r] < 2: u[r, h + 11, h, 0] = k
            if o[r] < 3: u[r, h + 8, h] = k
            else:
                u[r, h + 8, h, 0] = k
                u[r, h + 9, h, 0] = 1.125 * k
                u[r, h + 12, h, 0] = k
    return {"x": x.reshape(N, 128, 4 * C).astype(BF), "u": u.reshape(N, 128, 512), "v": d["v"], **stored(*orders(rng)), **weights(rng, w)}
def setup_inputs_odd(rng):
    d = numbers_of(rng)
    w = layers(rng, [0, 8])
    x = (1.0 + (2 * rng.integers(0, 64, (N, 16, 8, C, 4)) + 1) * 2.0 ** -7) * np.exp2(-rng.integers(0, 7, (N, 16, 8, C, 4)).astype(np.float64)) * rng.choice([-1.0, 1.0], (N, 16, 8, C, 4))
    x[:, 0::2, 0, :, 0] = 1.96875 * 2.0 ** 8 * rng.choice([-1.0, 1.0], (8, 1))
    x[:, 1::2, 0, :, 0] = rng.choice([1.96875 * 2.0 ** 8, 8.0], (N, 8, C)) * rng.choice([-1.0, 1.0], (N, 8, C))
    for g in range(8): w[:, g, 0, 0, g, 0, 0] = -0.5
    u = d["u"].reshape(N, 16, 8, 128, 4)
    u[:, :, 0, ::16] = 0
    for r in rng.permutation(N)[:N // 2]:
        for i, g in enumerate(rng.permutation(8)[:4]):
            x[r, 2 * g, 1, :, 0] = (8 + rng.integers(0, 2, C)) * 2.0 ** (i - 8)
            u[r, :, :, 16 * g] = 0
            u[r, 2 * g, 1, 16 * g, 0] = 1.0
            w[r, :, :, 0, g, 1] = 0
    return {"x": x.astype(np.float32).reshape(N, 128, 4 * C).astype(BF), "u": u.reshape(N, 128, 512), "v": d["v"], **stored(*orders(rng)), **weights(rng, w)}
def setup_inputs_ends(rng):
    d = numbers_of(rng)
    k, t = orders(rng)
    o, e, m = rng.permutation(N) % 4, rng.permutation(N) % 4, rng.permutation(N) % 4
    for r in range(N):
        s = (r - STEP[-1]) % N
        if o[r] == 3 and o[s] == 2:
            a = rng.choice([n for n in range(N) if o[n] < 2 and o[(n + STEP[-1]) % N] != 3])
            o[s] = o[a]
            o[a] = 2
    i = np.arange(C)
    k[e == 0] = i
    k[e == 1] = (i + 1) % C
    k[e == 2] = C - 1 - i
    k[e == 3] = (i - 1) % C
    t[m == 0] = i
    t[m == 1] = C - 1 - i
    t[m == 2] = i ^ 1
    x = np.zeros((N, 8, 16, C, 4))
    u = d["u"].astype(np.float32).reshape(N, 128, 128, 4)
    v = d["v"].astype(np.float32)
    w = np.zeros((N, 128, 4, 128, 4), np.float32)
    j = np.arange(128)
    for r in range(N):
        h = rng.permutation(8)
        c = np.where(h < 2, 0.0, h % 2 * 2.0 - 1.0)[None, :, None]
        low = -(0.7 + 0.1 * rng.random((8, 16, C, 4))) * 2.0 ** 30
        if o[r] == 0: x[r] = low
        if o[r] == 1: x[r] = low * rng.choice([-1.0, 1.0], (C, 1))
        if o[r] == 2: x[r] = -(1.0 + 0.125 * rng.integers(0, 8, (8, 16, C, 4))) * 2.0 ** -30
        if o[r] == 3: x[r] = d["x"][r].astype(np.float32).reshape(8, 16, C, 4)[:, :, :1]
        if o[r] < 2:
            u[r, :, ::16] = c * (0.9 + 0.1 * rng.random((128, 8, 4))) * 2.0 ** 30
            v[r] = rng.choice([-1.0, 1.0], (128, 512)) * (0.9 + 0.1 * rng.random((128, 512))) * 2.0 ** 30
        if o[r] == 2:
            u[r, :, ::16] = c * (1.0 + 0.125 * rng.integers(0, 8, (128, 8, 4))) * 2.0 ** -30
            v[r] = rng.choice([-1.0, 1.0], (128, 512)) * (1.0 + 0.125 * rng.integers(0, 8, (128, 512))) * 2.0 ** -30
        if o[r] == 3: u[r, :, ::16] *= np.abs(c).astype(np.float32)
        a = np.array([2.0, 2.0 ** -8, -0.25])[rng.permutation(8) % 3][j // 16]
        if o[r] == 2: a = np.zeros(128)
        a[120:] = 256.0
        for b in range(4): w[r, j, b, j, b] = a
    x[:, 7, 8:] = -2.0 ** -30
    return {"x": x.astype(np.float32).reshape(N, 128, 4 * C).astype(BF), "u": u.reshape(N, 128, 512).astype(BF), "v": v.astype(BF), **stored(k, t), **weights(rng, w.astype(BF))}
def setup_inputs_spread(rng):
    d = setup_inputs(rng)
    d["x"] = wide(rng, N, 128, 4 * C, cols=6)
    return d
def check_inputs(d):
    b = []
    for k in ("x", "u", "v"):
        a = np.abs(d[k].astype(np.float32))
        if not (np.isfinite(a).all() and ((a == 0) | (a >= 2.0 ** -30) & (a <= 2.0 ** 30)).all()): b.append("a value of " + k)
    none, least, most = [emit(mx_ref.quantize(np.full((128, 16), k, np.float32).astype(BF)))[1][0, 0] for k in (0.0, 2.0 ** -8, 2.0 ** 8)]
    for r in range(N):
        k, t = gentries(d["nx"][r]), gentries(d["mt"][r])
        if not (np.sort(k, axis=1) == np.arange(C)).all(): b.append("nx: not every column once")
        if not (((t >= 0) & (t < C)).all() and (np.take_along_axis(t, np.clip(t, 0, C - 1), axis=1) == np.arange(C)).all()): b.append("mt: not each other's")
        if ((d["wc"][r] == 0x7F) | (d["wc"][r] == 0xFF)).any(): b.append("wc: a code that is no number")
        s = mx_ref.live(d["ws"][r])
        if ((s != none) & ((s < least) | (s > most))).any(): b.append("ws: a scale out of range")
        if (((d["wc"][r].reshape(16, 8, 512, 4) & 0x7F) != 0) & (s == none)[:, None, :, None]).any(): b.append("wc: a code other than zero under the scale of zeros")
    return b
def at(a, e):
    return np.take_along_axis(a, e, axis=1)
def search(s, follow):
    b = np.tile(np.arange(C), (8, 1))
    p, left = b.copy(), np.ones((8, C), bool)
    for hop in range(1, HOPS + 1):
        to = at(follow, p)
        larger = left & (at(s, to) > s)
        b = np.where(larger, to, b)
        left = left & ~larger
        if hop < HOPS: p = np.where(left, to, p)
    return b, p
def layer(w, q):
    return tile([mx_ref.matmul(pick(w, np.arange(128 * k, 128 * k + 128)), q) * np.float32(0.03125) for k in range(4)])
def reference(x, u, v, nx, mt, wc, ws):
    qu = [mx_ref.quantize(u[r]) for r in range(N)]
    lay = [pk(wc[r], ws[r]) for r in range(N)]
    follow, mate = [gentries(nx[r]) for r in range(N)], [gentries(mt[r]) for r in range(N)]
    now = [x[r] for r in range(N)]
    for step in STEP:
        t, z, first = [], [], []
        for r in range(N):
            q = mx_ref.quantize(now[r])
            s = mx_ref.matmul(qu[r], q)[::16] + np.float32(0.0)
            b, p = search(s, follow[r])
            t.append(decode(q))
            c = t[r].astype(BF)
            z.append(mx_ref.quantize(((gcols(c, b).astype(np.float32) + gcols(c, p).astype(np.float32)) * np.float32(0.5)).astype(BF)))
            first.append(b)
            e = at(s, b)
            swap = at(e, np.minimum(mate[r], np.arange(C))) > at(e, np.maximum(mate[r], np.arange(C)))
            follow[r] = np.where(swap, at(follow[r], mate[r]), follow[r])
        now = [(t[r] + gcols(layer(lay[r], z[(r - step) % N]), first[r]).astype(np.float32)).astype(BF) for r in range(N)]
    y, nf = np.zeros((N, 128, C), np.float32), np.zeros((N, 8, C), np.float32)
    oc, osc = np.zeros((N, 128, 4 * C), np.uint8), np.zeros((N, 16, C), np.uint8)
    for r in range(N):
        q = mx_ref.quantize(now[r])
        y[r] = mx_ref.matmul(mx_ref.quantize(v[r]), q)
        nf[r] = follow[r]
        oc[r], osc[r] = emit(q)
    return {"y": y, "nf": nf, "oc": oc, "osc": osc}

@@ -1,0 +1,375 @@
+from concourse.mybir import dt, AluOpType, ActivationFunctionType
+
+C = 288
+L = 18
+B4 = 4 * C
+HALF = 160
+STEP = [4, 1, 2]
+N = 8
+BIG = 1e29
+KB = 1024.0
+F32, BF, I32, U16, F8, U8 = "float32", "bfloat16", "int32", "uint16", "float8_e4m3fn_x4", "uint8"
+
+
+def _scratch():
+    s = {}
+
+    def sb(names, n, d):
+        for k in names.split():
+            s[k] = ("sbuf", [128, n], d)
+    sb("pidx pi15", 1, I32)
+    sb("icol kj kb2", 1, F32)
+    sb("j16 dd k1 kk pen pen0 idt sc sp jg0 jg1 sj e1 e2 yo n0 n1 m0 m1 m2 m3 m4 m5 m6 h0 h1 h2 h3 h4 h5 h6", C, F32)
+    sb("kb kb1 kbt rm cc sm", C, BF)
+    sb("cl c0k posk dl el bitl fk fmf dsix mtf mnf mxf nxf", L, F32)
+    sb("nxi mti", L, I32)
+    sb("mnl mxl mtl jl0 jl1 jl2 jl3 jl4 jl5 pl0 pl1", L, U16)
+    sb("lst0 lst1 lst2 rl0 rl1 rl2 rr0 rr1 rr2", 2 * L, U16)
+    sb("uoi", 8, I32)
+    sb("uoff", 8, U16)
+    sb("ones wide", 516, BF)
+    sb("ut vt", 512, BF)
+    sb("x0 xt fo fz zp zt hh", B4, BF)
+    for k, n in (("uq", 128), ("u2", 128), ("vq", 128), ("ec", 512), ("wl", 512), ("zq", C)):
+        s[k] = ("sbuf", [128, n], F8)
+        s[k + "s"] = ("sbuf", [128, n], U8)
+    for t in range(4):
+        s["xq%d" % t] = ("sbuf", [128, C], F8)
+        s["xs%d" % t] = ("sbuf", [128, C], U8)
+    for t in range(3):
+        for a in "lr":
+            s[a + "c%d" % t] = ("sbuf", [128, C], F8)
+            s[a + "p%d" % t] = ("sbuf", [128, C], U8)
+    s["ps"] = ("psum", [128, 4096], F32)
+    return s
+
+
+SCRATCH = _scratch()
+SEMAPHORES = ["sv", "ss", "st", "sg", "ls", "out",
+              "dx", "du", "dv", "dwc", "dws", "dn", "dm"] + [a + str(t) for t in range(3) for a in ("rx", "rs")]
+
+
+def relay_of(topo, cores, a, b):
+    if topo.may_write(a, b):
+        return None
+    for q in topo.cores_of(a):
+        if q not in cores and topo.die(q) == topo.die(a) and topo.may_write(q, b):
+            return q
+    return None
+
+
+def targets(topo, cores, core):
+    out = []
+    for d in STEP:
+        for r in range(N):
+            a, b = cores[r], cores[(r + d) % N]
+            q = relay_of(topo, cores, a, b)
+            if a == core:
+                out.append(b if q is None else q)
+            elif q == core:
+                out.append(b)
+    return out
+
+
+def common_mask(topo, cores, core):
+    m = None
+    for b in targets(topo, cores, core):
+        m = topo.mask(core, b) if m is None else m & topo.mask(core, b)
+    return m
+
+
+def count(m):
+    n = 0
+    while m:
+        n += m & 1
+        m >>= 1
+    return n
+
+
+def rank_program(g, core, T, topo):
+    cores = list(T.cores)
+    rank = T.rank_of(core)
+    todo = targets(topo, cores, core)
+    if not todo:
+        return
+    mask = common_mask(topo, cores, core)
+    nsent = [0]
+
+    def send(dst, out, src, sem):
+        rid, pid = topo.addr(dst, core)
+        g.remote_dma(out, src, T.sem[sem], T.sem.ls, pid, rid, mask)
+        nsent[0] += count(mask)
+
+    def sender_count(src):
+        return count(common_mask(topo, cores, src))
+
+    if rank is None:
+        for t, d in enumerate(STEP):
+            for r in range(N):
+                a, b = cores[r], cores[(r + d) % N]
+                if relay_of(topo, cores, a, b) != core:
+                    continue
+                n = sender_count(a)
+                g.wait_ge(T.sem["rx%d" % t], 2 * n)
+                send(b, T["lc%d" % t][:, 0:C].bitcast(dt.uint8), T["rc%d" % t][:, 0:C].bitcast(dt.uint8), "rx%d" % t)
+                send(b, T["lp%d" % t][:, 0:C], T["rp%d" % t][:, 0:C], "rx%d" % t)
+                g.wait_ge(T.sem["rs%d" % t], n)
+                send(b, T["rl%d" % t][:, 0:2 * L], T["rr%d" % t][:, 0:2 * L], "rs%d" % t)
+        g.wait_ge(T.sem.ls, nsent[0])
+        return
+
+    A = AluOpType
+    COPY = ActivationFunctionType.Copy
+    queues = {"v": g.vector, "s": g.scalar, "t": g.tensor, "g": g, "y": g.sync}
+    semname = {"v": "sv", "s": "ss", "t": "st", "g": "sg"}
+    cnt = {"v": 0, "s": 0, "t": 0, "g": 0}
+    seen, wrote, readers = {}, {}, {}
+
+    def wait(q, sem, n):
+        if seen.get((q, sem), 0) < n:
+            queues[q].wait_ge(T.sem[sem], n)
+            seen[(q, sem)] = n
+
+    def before(q, reads, writes):
+        need = {}
+        for k in reads + writes:
+            if k in wrote:
+                s, n = wrote[k]
+                need[s] = max(need.get(s, 0), n)
+        for k in writes:
+            for s, n in readers.get(k, {}).items():
+                need[s] = max(need.get(s, 0), n)
+        for s, n in need.items():
+            wait(q, s, n)
+
+    def op(q, writes, reads, fn, *args, **kw):
+        writes, reads = writes.split(), reads.split()
+        before(q, reads, writes)
+        cnt[q] += 1
+        fn(*args, **kw).then_inc(T.sem[semname[q]], 1)
+        for k in reads:
+            readers.setdefault(k, {})[semname[q]] = cnt[q]
+        for k in writes:
+            wrote[k] = (semname[q], cnt[q])
+            readers[k] = {}
+
+    V, S, P = g.vector, g.scalar, g.tensor
+    ts, tt, tc, scan = V.tensor_scalar, V.tensor_tensor, V.tensor_copy, V.tensor_tensor_scan
+
+    def load(q, name, out, src, sem):
+        queues[q].dma_start(out, src).then_inc(T.sem[sem], 16)
+        wrote[name] = (sem, 16)
+
+    nout = [0]
+
+    def store(q, reads, out, src):
+        before(q, reads.split(), [])
+        queues[q].dma_start(out, src).then_inc(T.sem.out, 16)
+        nout[0] += 16
+
+    def bank(b, n=C):
+        return T.ps[:, 512 * b:512 * b + n]
+
+    load("y", "x0", T.x0[:], T.x[:], "dx")
+    load("s", "nxi", T.nxi[:], T.nx[:], "dn")
+    load("s", "ut", T.ut[:], T.u[:], "du")
+    load("s", "mti", T.mti[:], T.mt[:], "dm")
+    load("y", "wl", T.wl[:, 0:512].bitcast(dt.uint8), T.wc[:, 0:2048], "dwc")
+    load("y", "wls", T.wls[:, 0:512], T.ws[:, 0:512], "dws")
+    load("y", "vt", T.vt[:], T.v[:], "dv")
+
+    op("g", "pidx", "", g.iota, T.pidx[:], [[0, 1]], 0, 1)
+    op("g", "dl", "", g.iota, T.dl[:], [[16, L]], 0, 0, allow_small_or_imprecise_dtypes=True)
+    op("g", "j16", "", g.iota, T.j16[:], [[0, L], [1, 16]], 0, 0, allow_small_or_imprecise_dtypes=True)
+    op("g", "uoi", "", g.iota, T.uoi[:], [[16, 8]], 0, 0)
+    op("g", "idt", "", g.iota, T.idt[:], [[1, C]], 0, 0, allow_small_or_imprecise_dtypes=True)
+    op("v", "ones", "", V.memset, T.ones[:], 1.0)
+    op("g", "wide", "ones", g.affine_select, T.wide[:], T.ones[:], [[-1, 516]], A.is_equal, 0.0, 3, 4)
+    op("v", "pi15", "pidx", ts, T.pi15[:], T.pidx[:], 15, None, A.bitwise_and)
+    op("v", "icol", "pi15", tc, T.icol[:], T.pi15[:])
+    op("v", "kj", "icol", ts, T.kj[:], T.icol[:], 15.0, KB, A.is_lt, A.mult)
+    op("v", "kb2", "icol", ts, T.kb2[:], T.icol[:], 15.0, 2.0, A.is_lt, A.mult)
+    op("v", "cl", "dl icol", ts, T.cl[:], T.dl[:], T.icol[:, 0:1], None, A.add)
+    op("v", "c0k", "cl kj", ts, T.c0k[:], T.cl[:], T.kj[:, 0:1], None, A.add)
+    op("v", "dd", "j16 icol", ts, T.dd[:], T.j16[:], T.icol[:, 0:1], None, A.subtract)
+    op("v", "k1", "dd", ts, T.k1[:], T.dd[:], 0.0, -4.0 * KB, A.is_equal, A.mult)
+    op("v", "pen0", "dd", ts, T.pen0[:], T.dd[:], 1.0, KB, A.is_equal, A.mult)
+    op("v", "kk", "k1 pen0", tt, T.kk[:], T.k1[:], T.pen0[:], A.add)
+    op("v", "jl0", "nxi", tc, T.jl0[:], T.nxi[:])
+    op("v", "nxf", "nxi", tc, T.nxf[:], T.nxi[:])
+    kj, kb2 = T.kj[:, 0:1], T.kb2[:, 0:1]
+    op("v", "fk", "nxf kj", ts, T.fk[:], T.nxf[:], kj, None, A.add)
+
+    last = T.sj[:, 15:C:16]
+    lastm = T.sm[:, 15:C:16]
+
+    def ind(buf, lst, a=0):
+        return buf[:, a:a + C].indirect(lst)
+
+    def jl(k):
+        return T["jl%d" % k][:, 0:L]
+
+    def keep(src):
+        op("v", "sj", "kk " + src, scan, T.sj[:], T.kk[:], T[src][:], 0.0, A.add, A.max)
+
+    def hop0():
+        op("s", "h0", "idt jl0", S.activation, T.h0[:], ind(T.idt, jl(0)), COPY)
+
+    def hop(k):
+        op("s", "h%d" % k, "h%d jl%d" % (k - 1, k - 1), S.activation, T["h%d" % k][:], ind(T["h%d" % (k - 1)], jl(k - 1)), COPY)
+        if k < 6:
+            keep("h%d" % k)
+            op("v", "jl%d" % k, "sj kj", ts, jl(k), last, kj, None, A.subtract)
+
+    def quantize_x(t):
+        src = "x0" if t == 0 else "xt"
+        op("v", "xq%d" % t, "xt0 xt1 xt2 xt3" if t else "x0", V.quantize_mx,
+           T["xq%d" % t][:, 0:C], T["xs%d" % t][:, 0:C], T[src][:, 0:B4])
+
+    hop0()
+    hop(1)
+    op("v", "uq", "ut", V.quantize_mx, T.uq[:, 0:128], T.uqs[:, 0:128], T.ut[:, 0:512])
+    op("v", "uoff", "uoi", tc, T.uoff[:], T.uoi[:])
+    op("v", "u2", "uq uoff", tc, T.u2[:, 0:128].bitcast(dt.uint32), T.uq[:, 0:128].bitcast(dt.uint32).indirect(T.uoff[:, 0:8]))
+    op("v", "u2s", "uq uoff", tc, T.u2s[:, 0:128], T.uqs[:, 0:128].indirect(T.uoff[:, 0:8]))
+    hop(2)
+    op("v", "e1", "dd", ts, T.e1[:], T.dd[:], 0.0, 2.0 * BIG, A.is_equal, A.mult)
+    op("v", "pen", "e1", ts, T.pen[:], T.e1[:], -BIG, None, A.add)
+    op("v", "rm", "j16", ts, T.rm[:], T.j16[:], 0.0, None, A.not_equal)
+    op("v", "kb1", "dd", ts, T.kb1[:], T.dd[:], 0.0, -8.0, A.is_equal, A.mult)
+    op("v", "kbt", "dd", ts, T.kbt[:], T.dd[:], 1.0, 2.0, A.is_equal, A.mult)
+    op("v", "kb", "kb1 kbt", tt, T.kb[:], T.kb1[:], T.kbt[:], A.add)
+    quantize_x(0)
+    hop(3)
+    for b in range(4):
+        op("v", "ec%d" % b, "wide", V.quantize_mx, T.ec[:, 128 * b:128 * b + 128], T.ecs[:, 128 * b:128 * b + 128], T.wide[:, 3 - b:515 - b])
+    hop(4)
+    op("v", "mtf", "mti", tc, T.mtf[:], T.mti[:])
+    op("v", "mtl", "mti", tc, T.mtl[:], T.mti[:])
+    op("v", "mnf", "mtf cl", tt, T.mnf[:], T.mtf[:], T.cl[:], A.min)
+    op("v", "mxf", "mtf cl", tt, T.mxf[:], T.mtf[:], T.cl[:], A.max)
+    op("v", "mnl", "mnf", tc, T.mnl[:], T.mnf[:])
+    op("v", "mxl", "mxf", tc, T.mxl[:], T.mxf[:])
+    hop(5)
+
+    def product(b, lhs, ls, a, rhs, rs, reads):
+        op("t", "b%d" % b, reads, P.matmul_mx, bank(b), lhs[:, a:a + 128], ls[:, a:a + 128], rhs[:, 0:C], rs[:, 0:C], True, True)
+
+    def plane(buf, b):
+        return buf[:, C * b:C * b + C]
+
+    for t, d in enumerate(STEP):
+        to, frm = cores[(rank + d) % N], cores[(rank - d) % N]
+        via, came = relay_of(topo, cores, core, to), relay_of(topo, cores, frm, core)
+        xq, xs = T["xq%d" % t], T["xs%d" % t]
+        if t:
+            quantize_x(t)
+        before("g", ["xq%d" % t], [])
+        nxt, lc, lp, ll = (to, "lc%d", "lp%d", "rl%d") if via is None else (via, "rc%d", "rp%d", "rr%d")
+        send(nxt, T[lc % t][:, 0:C].bitcast(dt.uint8), xq[:, 0:C].bitcast(dt.uint8), "rx%d" % t)
+        send(nxt, T[lp % t][:, 0:C], xs[:, 0:C], "rx%d" % t)
+        n = sender_count(frm if came is None else came)
+        wrote["land"], wrote["rl"] = ("rx%d" % t, 2 * n), ("rs%d" % t, n)
+        product(0, T.u2, T.u2s, 0, xq, xs, "u2 u2s xq%d" % t)
+        product(1, T.u2, T.u2s, 0, xq, xs, "u2 u2s xq%d" % t)
+        for b in range(4):
+            product(2 + b, T.ec, T.ecs, 128 * b, xq, xs, "ec%d xq%d" % (b, t))
+        hop(6)
+        op("s", "jg0", "h0 mtl", S.activation, T.jg0[:], ind(T.h0, T.mtl[:, 0:L]), COPY)
+        op("s", "sc", "b0", S.activation, T.sc[:], bank(0), COPY)
+        keep("h6")
+        op("v", "dsix", "sj c0k", tt, T.dsix[:], last, T.c0k[:], A.subtract)
+        keep("jg0")
+        op("v", "fmf", "sj fk", tt, T.fmf[:], last, T.fk[:], A.subtract)
+        op("v", "sp", "b1 pen", tt, T.sp[:], bank(1), T.pen[:], A.min)
+        op("s", "n0a n0b", "sc jl0", S.activation, T.n0[:], ind(T.sc, jl(0)), COPY)
+        op("v", "m0", "sc jl0", tc, T.m0[:], ind(T.sc, jl(0)))
+        for k in range(6):
+            m, m2, n1, n2 = "m%d" % k, "m%d" % (k + 1), "n%d" % (k % 2), "n%d" % ((k + 1) % 2)
+            op("v", m2, "%s jl%d %sa %sb" % (m, k, n1, n1), tt, T[m2][:], ind(T[m], jl(k)), T[n1][:], A.max)
+            if k < 5:
+                op("v", n2 + "a", m2, tc, T[n2][:, 0:HALF], T[m2][:, 0:HALF])
+                op("s", n2 + "b", m2, S.activation, T[n2][:, HALF:C], T[m2][:, HALF:C], COPY)
+        op("v", "cc", "m6 b1", tt, T.cc[:], T.m6[:], bank(1), A.is_le)
+        op("v", "sm", "kb cc", scan, T.sm[:], T.kb[:], T.cc[:], 0.0, A.add, A.max)
+        op("v", "bitl", "sm kb2", ts, T.bitl[:], lastm, kb2, None, A.subtract)
+        op("v", "el", "bitl dsix", tt, T.el[:], T.bitl[:], T.dsix[:], A.mult)
+        op("v", "posk", "c0k el", tt, T.posk[:], T.c0k[:], T.el[:], A.add)
+        op("v", "pl0", "posk kj", ts, T.pl0[:], T.posk[:], kj, None, A.subtract)
+        lst = T["lst%d" % t]
+        at, key = T.pl0[:, 0:L], "pl0"
+        for k in [5, 4, 3, 2, 1, 0, -1]:
+            i, jg = max(k, 0), "jg%d" % (k % 2)
+            op("s", jg, "h%d %s" % (i, key), S.activation, T[jg][:], ind(T["h%d" % i], at), COPY)
+            op("v", "cc", "m%d sp %s" % (i, key), tt, T.cc[:], ind(T["m%d" % i], at), T.sp[:], A.is_le)
+            if 2 <= k <= 5:
+                b = 5 - k
+                op("s", "fo%d" % b, "b%d" % (2 + b), S.activation, plane(T.fo, b), bank(2 + b), COPY)
+                product(2 + b, T.ec, T.ecs, 128 * b, T["lc%d" % t], T["lp%d" % t], "land ec%d" % b)
+            op("v", "sm", "rm cc", scan, T.sm[:], T.rm[:], T.cc[:], 0.0, A.mult, A.add)
+            keep(jg)
+            if k >= 0:
+                op("v", "dl", "sj posk", tt, T.dl[:], last, T.posk[:], A.subtract)
+                op("v", "el", "sm dl", tt, T.el[:], lastm, T.dl[:], A.mult)
+                op("v", "posk", "posk el", tt, T.posk[:], T.posk[:], T.el[:], A.add)
+            else:
+                op("v", "dl", "sj c0k", tt, T.dl[:], T.c0k[:], last, A.subtract)
+                op("v", "el", "sm dl", tt, T.el[:], lastm, T.dl[:], A.mult)
+                op("v", "posk", "sj el", tt, T.posk[:], last, T.el[:], A.add)
+            if k > 0:
+                key = "pl%d" % (k % 2)
+                at = T[key][:, 0:L]
+            elif k == 0:
+                key, at = "lstp", lst[:, L:2 * L]
+            else:
+                key, at = "lstb", lst[:, 0:L]
+            op("v", key, "posk kj", ts, at, T.posk[:], kj, None, A.subtract)
+        before("g", ["lstb", "lstp"], [])
+        send(nxt, T[ll % t][:, 0:2 * L], lst[:, 0:2 * L], "rs%d" % t)
+        bl = lst[:, 0:L]
+        for b in range(4):
+            op("s", "fz%d" % b, "b%d" % (2 + b), S.activation, plane(T.fz, b), bank(2 + b), COPY, scale=0.5)
+        op("v", "e1", "sc lstb", tc, T.e1[:], ind(T.sc, bl))
+        op("v", "e2", "e1 mxl", tc, T.e2[:], ind(T.e1, T.mxl[:, 0:L]))
+        op("v", "cc", "e1 e2 mnl", tt, T.cc[:], ind(T.e1, T.mnl[:, 0:L]), T.e2[:], A.is_gt)
+        op("v", "sm", "kb cc", scan, T.sm[:], T.kb[:], T.cc[:], 0.0, A.add, A.max)
+        op("v", "bitl", "sm kb2", ts, T.bitl[:], lastm, kb2, None, A.subtract)
+        op("v", "el", "bitl fmf", tt, T.el[:], T.bitl[:], T.fmf[:], A.mult)
+        op("v", "fk", "fk el", tt, T.fk[:], T.fk[:], T.el[:], A.add)
+        op("v", "jl0", "fk kj", ts, jl(0), T.fk[:], kj, None, A.subtract)
+        hop0()
+        if t < 2:
+            for k in (1, 2, 3):
+                hop(k)
+        else:
+            for i in range(8):
+                store("y", "h0", T.nf[i:i + 1, :], T.h0[16 * i:16 * i + 1, :])
+        rl = T["rl%d" % t]
+        for b in range(4):
+            op("s", "zp%d" % b, "fz%d rl" % b, S.activation, plane(T.zp, b), ind(T.fz, rl[:, L:2 * L], C * b), COPY)
+        for b in range(4):
+            op("v", "zt%d" % b, "fz%d zp%d rl" % (b, b), tt, T.zt[:, b:B4:4], ind(T.fz, rl[:, 0:L], C * b), plane(T.zp, b), A.add)
+        op("v", "zq", "zt0 zt1 zt2 zt3", V.quantize_mx, T.zq[:, 0:C], T.zqs[:, 0:C], T.zt[:, 0:B4])
+        hb = [6, 7, 2, 3]
+        for b in range(4):
+            product(hb[b], T.wl, T.wls, 128 * b, T.zq, T.zqs, "wl wls zq")
+        if t < 2:
+            hop(4)
+            hop(5)
+        for b in range(4):
+            op("s", "hh%d" % b, "b%d" % hb[b], S.activation, plane(T.hh, b), bank(hb[b]), COPY, scale=0.03125)
+        for b in range(4):
+            op("v", "xt%d" % b, "hh%d fo%d lstb" % (b, b), tt, T.xt[:, b:B4:4], ind(T.hh, bl, C * b), plane(T.fo, b), A.add)
+        if t == 0:
+            op("v", "vq", "vt", V.quantize_mx, T.vq[:, 0:128], T.vqs[:, 0:128], T.vt[:, 0:512])
+    quantize_x(3)
+    product(0, T.vq, T.vqs, 0, T.xq3, T.xs3, "vq xq3")
+    store("y", "xq3", T.oc[:, 0:B4], T.xq3[:, 0:C].bitcast(dt.uint8))
+    op("v", "yo", "b0", tc, T.yo[:], bank(0))
+    for k in range(4):
+        store("s", "xq3", T.osc[4 * k:4 * k + 4, 0:C], T.xs3[32 * k:32 * k + 4, 0:C])
+    store("y", "yo", T.y[:], T.yo[:])
+    for q in ("v", "s", "t", "g"):
+        wait("g", semname[q], cnt[q])
+    wait("g", "ls", nsent[0])
+    wait("g", "out", nout[0])

@@ -3,7 +3,6 @@ from concourse.mybir import dt, AluOpType, ActivationFunctionType
 C = 288
 L = 18
 B4 = 4 * C
-HALF = 160
 STEP = [4, 1, 2]
 N = 8
 BIG = 1e29
@@ -19,9 +18,9 @@ def _scratch():
             s[k] = ("sbuf", [128, n], d)
     sb("pidx pi15", 1, I32)
     sb("icol kj kb2", 1, F32)
-    sb("j16 dd k1 kk pen pen0 idt sc sp jg0 jg1 sj e1 e2 yo n0 n1 m0 m1 m2 m3 m4 m5 m6 h0 h1 h2 h3 h4 h5 h6", C, F32)
-    sb("kb kb1 kbt rm cc sm", C, BF)
-    sb("cl c0k posk dl el bitl fk fmf dsix mtf mnf mxf nxf", L, F32)
+    sb("j16 dd kk pen idt sc sp jg0 jg1 sj e1 e2 sk yo n0 n1 m0 m1 m2 m3 m4 m5 m6 m7 h0 h1 h2 h3 h4 h5 h6", C, F32)
+    sb("kb rm cc sm cc2 sm2", C, BF)
+    sb("cl c0k posk dl el dl2 el2 dl3 bitl fk fmf dsix csix mtf mnf mxf", L, F32)
     sb("nxi mti", L, I32)
     sb("mnl mxl mtl jl0 jl1 jl2 jl3 jl4 jl5 pl0 pl1", L, U16)
     sb("lst0 lst1 lst2 rl0 rl1 rl2 rr0 rr1 rr2", 2 * L, U16)
@@ -71,37 +70,18 @@ def targets(topo, cores, core):
     return out
 
 
-def common_mask(topo, cores, core):
-    m = None
-    for b in targets(topo, cores, core):
-        m = topo.mask(core, b) if m is None else m & topo.mask(core, b)
-    return m
-
-
-def count(m):
-    n = 0
-    while m:
-        n += m & 1
-        m >>= 1
-    return n
-
-
 def rank_program(g, core, T, topo):
     cores = list(T.cores)
     rank = T.rank_of(core)
     todo = targets(topo, cores, core)
     if not todo:
         return
-    mask = common_mask(topo, cores, core)
     nsent = [0]
 
     def send(dst, out, src, sem):
         rid, pid = topo.addr(dst, core)
-        g.remote_dma(out, src, T.sem[sem], T.sem.ls, pid, rid, mask)
-        nsent[0] += count(mask)
-
-    def sender_count(src):
-        return count(common_mask(topo, cores, src))
+        g.remote_dma(out, src, T.sem[sem], T.sem.ls, pid, rid, topo.mask(core, dst))
+        nsent[0] += len(topo.engines(core, dst))
 
     if rank is None:
         for t, d in enumerate(STEP):
@@ -109,7 +89,7 @@ def rank_program(g, core, T, topo):
                 a, b = cores[r], cores[(r + d) % N]
                 if relay_of(topo, cores, a, b) != core:
                     continue
-                n = sender_count(a)
+                n = len(topo.engines(a, core))
                 g.wait_ge(T.sem["rx%d" % t], 2 * n)
                 send(b, T["lc%d" % t][:, 0:C].bitcast(dt.uint8), T["rc%d" % t][:, 0:C].bitcast(dt.uint8), "rx%d" % t)
                 send(b, T["lp%d" % t][:, 0:C], T["rp%d" % t][:, 0:C], "rx%d" % t)
@@ -192,13 +172,13 @@ def rank_program(g, core, T, topo):
     op("v", "cl", "dl icol", ts, T.cl[:], T.dl[:], T.icol[:, 0:1], None, A.add)
     op("v", "c0k", "cl kj", ts, T.c0k[:], T.cl[:], T.kj[:, 0:1], None, A.add)
     op("v", "dd", "j16 icol", ts, T.dd[:], T.j16[:], T.icol[:, 0:1], None, A.subtract)
-    op("v", "k1", "dd", ts, T.k1[:], T.dd[:], 0.0, -4.0 * KB, A.is_equal, A.mult)
-    op("v", "pen0", "dd", ts, T.pen0[:], T.dd[:], 1.0, KB, A.is_equal, A.mult)
-    op("v", "kk", "k1 pen0", tt, T.kk[:], T.k1[:], T.pen0[:], A.add)
+    op("v", "m0", "dd", ts, T.m0[:], T.dd[:], 0.0, -4.0 * KB, A.is_equal, A.mult)
+    op("v", "m1", "dd", ts, T.m1[:], T.dd[:], 1.0, KB, A.is_equal, A.mult)
+    op("v", "kk", "m0 m1", tt, T.kk[:], T.m0[:], T.m1[:], A.add)
     op("v", "jl0", "nxi", tc, T.jl0[:], T.nxi[:])
-    op("v", "nxf", "nxi", tc, T.nxf[:], T.nxi[:])
+    op("v", "dl2", "nxi", tc, T.dl2[:], T.nxi[:])
     kj, kb2 = T.kj[:, 0:1], T.kb2[:, 0:1]
-    op("v", "fk", "nxf kj", ts, T.fk[:], T.nxf[:], kj, None, A.add)
+    op("v", "fk", "dl2 kj", ts, T.fk[:], T.dl2[:], kj, None, A.add)
 
     last = T.sj[:, 15:C:16]
     lastm = T.sm[:, 15:C:16]
@@ -217,9 +197,15 @@ def rank_program(g, core, T, topo):
 
     def hop(k):
         op("s", "h%d" % k, "h%d jl%d" % (k - 1, k - 1), S.activation, T["h%d" % k][:], ind(T["h%d" % (k - 1)], jl(k - 1)), COPY)
+
+    def tolist(k):
+        keep("h%d" % k)
         if k < 6:
-            keep("h%d" % k)
             op("v", "jl%d" % k, "sj kj", ts, jl(k), last, kj, None, A.subtract)
+        else:
+            op("v", "dsix", "sj c0k", tt, T.dsix[:], last, T.c0k[:], A.subtract)
+            op("v", "dl", "dsix kb2", ts, T.dl[:], T.dsix[:], kb2, None, A.mult)
+            op("v", "csix", "c0k dl", tt, T.csix[:], T.c0k[:], T.dl[:], A.subtract)
 
     def quantize_x(t):
         src = "x0" if t == 0 else "xt"
@@ -232,25 +218,22 @@ def rank_program(g, core, T, topo):
     op("v", "uoff", "uoi", tc, T.uoff[:], T.uoi[:])
     op("v", "u2", "uq uoff", tc, T.u2[:, 0:128].bitcast(dt.uint32), T.uq[:, 0:128].bitcast(dt.uint32).indirect(T.uoff[:, 0:8]))
     op("v", "u2s", "uq uoff", tc, T.u2s[:, 0:128], T.uqs[:, 0:128].indirect(T.uoff[:, 0:8]))
-    hop(2)
     op("v", "e1", "dd", ts, T.e1[:], T.dd[:], 0.0, 2.0 * BIG, A.is_equal, A.mult)
     op("v", "pen", "e1", ts, T.pen[:], T.e1[:], -BIG, None, A.add)
     op("v", "rm", "j16", ts, T.rm[:], T.j16[:], 0.0, None, A.not_equal)
-    op("v", "kb1", "dd", ts, T.kb1[:], T.dd[:], 0.0, -8.0, A.is_equal, A.mult)
-    op("v", "kbt", "dd", ts, T.kbt[:], T.dd[:], 1.0, 2.0, A.is_equal, A.mult)
-    op("v", "kb", "kb1 kbt", tt, T.kb[:], T.kb1[:], T.kbt[:], A.add)
-    quantize_x(0)
-    hop(3)
-    for b in range(4):
-        op("v", "ec%d" % b, "wide", V.quantize_mx, T.ec[:, 128 * b:128 * b + 128], T.ecs[:, 128 * b:128 * b + 128], T.wide[:, 3 - b:515 - b])
-    hop(4)
+    op("v", "cc", "dd", ts, T.cc[:], T.dd[:], 0.0, -8.0, A.is_equal, A.mult)
+    op("v", "cc2", "dd", ts, T.cc2[:], T.dd[:], 1.0, 2.0, A.is_equal, A.mult)
+    op("v", "kb", "cc cc2", tt, T.kb[:], T.cc[:], T.cc2[:], A.add)
+    tolist(1)
     op("v", "mtf", "mti", tc, T.mtf[:], T.mti[:])
     op("v", "mtl", "mti", tc, T.mtl[:], T.mti[:])
     op("v", "mnf", "mtf cl", tt, T.mnf[:], T.mtf[:], T.cl[:], A.min)
     op("v", "mxf", "mtf cl", tt, T.mxf[:], T.mtf[:], T.cl[:], A.max)
     op("v", "mnl", "mnf", tc, T.mnl[:], T.mnf[:])
     op("v", "mxl", "mxf", tc, T.mxl[:], T.mxf[:])
-    hop(5)
+    quantize_x(0)
+    for b in range(4):
+        op("v", "ec%d" % b, "wide", V.quantize_mx, T.ec[:, 128 * b:128 * b + 128], T.ecs[:, 128 * b:128 * b + 128], T.wide[:, 3 - b:515 - b])
 
     def product(b, lhs, ls, a, rhs, rs, reads):
         op("t", "b%d" % b, reads, P.matmul_mx, bank(b), lhs[:, a:a + 128], ls[:, a:a + 128], rhs[:, 0:C], rs[:, 0:C], True, True)
@@ -268,70 +251,79 @@ def rank_program(g, core, T, topo):
         nxt, lc, lp, ll = (to, "lc%d", "lp%d", "rl%d") if via is None else (via, "rc%d", "rp%d", "rr%d")
         send(nxt, T[lc % t][:, 0:C].bitcast(dt.uint8), xq[:, 0:C].bitcast(dt.uint8), "rx%d" % t)
         send(nxt, T[lp % t][:, 0:C], xs[:, 0:C], "rx%d" % t)
-        n = sender_count(frm if came is None else came)
+        n = len(topo.engines(frm if came is None else came, core))
         wrote["land"], wrote["rl"] = ("rx%d" % t, 2 * n), ("rs%d" % t, n)
         product(0, T.u2, T.u2s, 0, xq, xs, "u2 u2s xq%d" % t)
         product(1, T.u2, T.u2s, 0, xq, xs, "u2 u2s xq%d" % t)
         for b in range(4):
             product(2 + b, T.ec, T.ecs, 128 * b, xq, xs, "ec%d xq%d" % (b, t))
-        hop(6)
-        op("s", "jg0", "h0 mtl", S.activation, T.jg0[:], ind(T.h0, T.mtl[:, 0:L]), COPY)
+        if t:
+            tolist(1)
         op("s", "sc", "b0", S.activation, T.sc[:], bank(0), COPY)
-        keep("h6")
-        op("v", "dsix", "sj c0k", tt, T.dsix[:], last, T.c0k[:], A.subtract)
-        keep("jg0")
-        op("v", "fmf", "sj fk", tt, T.fmf[:], last, T.fk[:], A.subtract)
         op("v", "sp", "b1 pen", tt, T.sp[:], bank(1), T.pen[:], A.min)
-        op("s", "n0a n0b", "sc jl0", S.activation, T.n0[:], ind(T.sc, jl(0)), COPY)
+        op("s", "n0", "sc jl0", S.activation, T.n0[:], ind(T.sc, jl(0)), COPY)
         op("v", "m0", "sc jl0", tc, T.m0[:], ind(T.sc, jl(0)))
         for k in range(6):
             m, m2, n1, n2 = "m%d" % k, "m%d" % (k + 1), "n%d" % (k % 2), "n%d" % ((k + 1) % 2)
-            op("v", m2, "%s jl%d %sa %sb" % (m, k, n1, n1), tt, T[m2][:], ind(T[m], jl(k)), T[n1][:], A.max)
+            op("v", m2, "%s jl%d %s" % (m, k, n1), tt, T[m2][:], ind(T[m], jl(k)), T[n1][:], A.max)
             if k < 5:
-                op("v", n2 + "a", m2, tc, T[n2][:, 0:HALF], T[m2][:, 0:HALF])
-                op("s", n2 + "b", m2, S.activation, T[n2][:, HALF:C], T[m2][:, HALF:C], COPY)
+                hop(k + 2)
+                op("s", n2, m2, S.activation, T[n2][:], T[m2][:], COPY)
+                tolist(k + 2)
+        op("s", "m7", "m0 jl0", S.activation, T.m7[:], ind(T.m0, jl(0)), COPY)
         op("v", "cc", "m6 b1", tt, T.cc[:], T.m6[:], bank(1), A.is_le)
         op("v", "sm", "kb cc", scan, T.sm[:], T.kb[:], T.cc[:], 0.0, A.add, A.max)
-        op("v", "bitl", "sm kb2", ts, T.bitl[:], lastm, kb2, None, A.subtract)
-        op("v", "el", "bitl dsix", tt, T.el[:], T.bitl[:], T.dsix[:], A.mult)
-        op("v", "posk", "c0k el", tt, T.posk[:], T.c0k[:], T.el[:], A.add)
+        op("v", "el", "sm dsix", tt, T.el[:], lastm, T.dsix[:], A.mult)
+        op("v", "posk", "csix el", tt, T.posk[:], T.csix[:], T.el[:], A.add)
         op("v", "pl0", "posk kj", ts, T.pl0[:], T.posk[:], kj, None, A.subtract)
         lst = T["lst%d" % t]
         at, key = T.pl0[:, 0:L], "pl0"
-        for k in [5, 4, 3, 2, 1, 0, -1]:
-            i, jg = max(k, 0), "jg%d" % (k % 2)
-            op("s", jg, "h%d %s" % (i, key), S.activation, T[jg][:], ind(T["h%d" % i], at), COPY)
-            op("v", "cc", "m%d sp %s" % (i, key), tt, T.cc[:], ind(T["m%d" % i], at), T.sp[:], A.is_le)
-            if 2 <= k <= 5:
+        for k in [5, 4, 3, 2, 1]:
+            jg = "jg%d" % (k % 2)
+            op("s", jg, "h%d %s" % (k, key), S.activation, T[jg][:], ind(T["h%d" % k], at), COPY)
+            op("v", "cc", "m%d sp %s" % (k, key), tt, T.cc[:], ind(T["m%d" % k], at), T.sp[:], A.is_le)
+            if k >= 2:
                 b = 5 - k
                 op("s", "fo%d" % b, "b%d" % (2 + b), S.activation, plane(T.fo, b), bank(2 + b), COPY)
                 product(2 + b, T.ec, T.ecs, 128 * b, T["lc%d" % t], T["lp%d" % t], "land ec%d" % b)
-            op("v", "sm", "rm cc", scan, T.sm[:], T.rm[:], T.cc[:], 0.0, A.mult, A.add)
             keep(jg)
-            if k >= 0:
-                op("v", "dl", "sj posk", tt, T.dl[:], last, T.posk[:], A.subtract)
-                op("v", "el", "sm dl", tt, T.el[:], lastm, T.dl[:], A.mult)
-                op("v", "posk", "posk el", tt, T.posk[:], T.posk[:], T.el[:], A.add)
-            else:
-                op("v", "dl", "sj c0k", tt, T.dl[:], T.c0k[:], last, A.subtract)
-                op("v", "el", "sm dl", tt, T.el[:], lastm, T.dl[:], A.mult)
-                op("v", "posk", "sj el", tt, T.posk[:], last, T.el[:], A.add)
-            if k > 0:
-                key = "pl%d" % (k % 2)
-                at = T[key][:, 0:L]
-            elif k == 0:
-                key, at = "lstp", lst[:, L:2 * L]
-            else:
-                key, at = "lstb", lst[:, 0:L]
+            op("v", "sm", "rm cc", scan, T.sm[:], T.rm[:], T.cc[:], 0.0, A.mult, A.add)
+            op("v", "dl", "sj posk", tt, T.dl[:], last, T.posk[:], A.subtract)
+            op("v", "el", "sm dl", tt, T.el[:], lastm, T.dl[:], A.mult)
+            op("v", "posk", "posk el", tt, T.posk[:], T.posk[:], T.el[:], A.add)
+            key = "pl%d" % (k % 2)
+            at = T[key][:, 0:L]
             op("v", key, "posk kj", ts, at, T.posk[:], kj, None, A.subtract)
+        op("s", "jg0", "h0 " + key, S.activation, T.jg0[:], ind(T.h0, at), COPY)
+        op("v", "cc", "m0 sp " + key, tt, T.cc[:], ind(T.m0, at), T.sp[:], A.is_le)
+        op("s", "jg1", "h1 " + key, S.activation, T.jg1[:], ind(T.h1, at), COPY)
+        op("v", "cc2", "m7 sp " + key, tt, T.cc2[:], ind(T.m7, at), T.sp[:], A.is_le)
+        keep("jg0")
+        op("v", "sm", "rm cc", scan, T.sm[:], T.rm[:], T.cc[:], 0.0, A.mult, A.add)
+        op("v", "sm2", "rm cc2", scan, T.sm2[:], T.rm[:], T.cc2[:], 0.0, A.mult, A.add)
+        op("v", "sk", "kk jg1", scan, T.sk[:], T.kk[:], T.jg1[:], 0.0, A.add, A.max)
+        op("v", "dl", "sj posk", tt, T.dl[:], last, T.posk[:], A.subtract)
+        op("v", "dl2", "sk c0k", tt, T.dl2[:], T.c0k[:], T.sk[:, 15:C:16], A.subtract)
+        op("v", "el", "sm dl", tt, T.el[:], lastm, T.dl[:], A.mult)
+        op("v", "el2", "sm2 dl2", tt, T.el2[:], T.sm2[:, 15:C:16], T.dl2[:], A.mult)
+        op("v", "dl3", "sk sj", tt, T.dl3[:], T.sk[:, 15:C:16], last, A.subtract)
+        op("v", "posk", "posk el", tt, T.posk[:], T.posk[:], T.el[:], A.add)
+        op("v", "el2", "el2 dl3", tt, T.el2[:], T.el2[:], T.dl3[:], A.add)
+        op("v", "el2", "el2 sm", tt, T.el2[:], T.el2[:], lastm, A.mult)
+        op("v", "lstp", "posk kj", ts, lst[:, L:2 * L], T.posk[:], kj, None, A.subtract)
+        op("v", "el2", "el2 sj", tt, T.el2[:], T.el2[:], last, A.add)
+        op("v", "lstb", "el2 kj", ts, lst[:, 0:L], T.el2[:], kj, None, A.subtract)
         before("g", ["lstb", "lstp"], [])
         send(nxt, T[ll % t][:, 0:2 * L], lst[:, 0:2 * L], "rs%d" % t)
         bl = lst[:, 0:L]
+        op("s", "jg0", "h0 mtl", S.activation, T.jg0[:], ind(T.h0, T.mtl[:, 0:L]), COPY)
         for b in range(4):
             op("s", "fz%d" % b, "b%d" % (2 + b), S.activation, plane(T.fz, b), bank(2 + b), COPY, scale=0.5)
         op("v", "e1", "sc lstb", tc, T.e1[:], ind(T.sc, bl))
         op("v", "e2", "e1 mxl", tc, T.e2[:], ind(T.e1, T.mxl[:, 0:L]))
         op("v", "cc", "e1 e2 mnl", tt, T.cc[:], ind(T.e1, T.mnl[:, 0:L]), T.e2[:], A.is_gt)
+        keep("jg0")
+        op("v", "fmf", "sj fk", tt, T.fmf[:], last, T.fk[:], A.subtract)
         op("v", "sm", "kb cc", scan, T.sm[:], T.kb[:], T.cc[:], 0.0, A.add, A.max)
         op("v", "bitl", "sm kb2", ts, T.bitl[:], lastm, kb2, None, A.subtract)
         op("v", "el", "bitl fmf", tt, T.el[:], T.bitl[:], T.fmf[:], A.mult)
@@ -339,8 +331,7 @@ def rank_program(g, core, T, topo):
         op("v", "jl0", "fk kj", ts, jl(0), T.fk[:], kj, None, A.subtract)
         hop0()
         if t < 2:
-            for k in (1, 2, 3):
-                hop(k)
+            hop(1)
         else:
             for i in range(8):
                 store("y", "h0", T.nf[i:i + 1, :], T.h0[16 * i:16 * i + 1, :])
@@ -353,9 +344,6 @@ def rank_program(g, core, T, topo):
         hb = [6, 7, 2, 3]
         for b in range(4):
             product(hb[b], T.wl, T.wls, 128 * b, T.zq, T.zqs, "wl wls zq")
-        if t < 2:
-            hop(4)
-            hop(5)
         for b in range(4):
             op("s", "hh%d" % b, "b%d" % hb[b], S.activation, plane(T.hh, b), bank(hb[b]), COPY, scale=0.03125)
         for b in range(4):

@@ -3,6 +3,7 @@ from concourse.mybir import dt, AluOpType, ActivationFunctionType
 C = 288
 L = 18
 B4 = 4 * C
+HALF = C // 2
 STEP = [4, 1, 2]
 N = 8
 BIG = 1e29
@@ -152,8 +153,10 @@ def rank_program(g, core, T, topo):
 
     load("y", "x0", T.x0[:], T.x[:], "dx")
     load("s", "nxi", T.nxi[:], T.nx[:], "dn")
-    load("s", "ut", T.ut[:], T.u[:], "du")
     load("s", "mti", T.mti[:], T.mt[:], "dm")
+    load("s", "ut", T.ut[:], T.u[:], "du")
+    wait("y", "dx", 16)
+    wait("y", "du", 16)
     load("y", "wl", T.wl[:, 0:512].bitcast(dt.uint8), T.wc[:, 0:2048], "dwc")
     load("y", "wls", T.wls[:, 0:512], T.ws[:, 0:512], "dws")
     load("y", "vt", T.vt[:], T.v[:], "dv")
@@ -214,29 +217,29 @@ def rank_program(g, core, T, topo):
 
     hop0()
     hop(1)
-    op("v", "uq", "ut", V.quantize_mx, T.uq[:, 0:128], T.uqs[:, 0:128], T.ut[:, 0:512])
-    op("v", "uoff", "uoi", tc, T.uoff[:], T.uoi[:])
-    op("v", "u2", "uq uoff", tc, T.u2[:, 0:128].bitcast(dt.uint32), T.uq[:, 0:128].bitcast(dt.uint32).indirect(T.uoff[:, 0:8]))
-    op("v", "u2s", "uq uoff", tc, T.u2s[:, 0:128], T.uqs[:, 0:128].indirect(T.uoff[:, 0:8]))
     op("v", "e1", "dd", ts, T.e1[:], T.dd[:], 0.0, 2.0 * BIG, A.is_equal, A.mult)
     op("v", "pen", "e1", ts, T.pen[:], T.e1[:], -BIG, None, A.add)
     op("v", "rm", "j16", ts, T.rm[:], T.j16[:], 0.0, None, A.not_equal)
     op("v", "cc", "dd", ts, T.cc[:], T.dd[:], 0.0, -8.0, A.is_equal, A.mult)
     op("v", "cc2", "dd", ts, T.cc2[:], T.dd[:], 1.0, 2.0, A.is_equal, A.mult)
     op("v", "kb", "cc cc2", tt, T.kb[:], T.cc[:], T.cc2[:], A.add)
-    tolist(1)
     op("v", "mtf", "mti", tc, T.mtf[:], T.mti[:])
     op("v", "mtl", "mti", tc, T.mtl[:], T.mti[:])
     op("v", "mnf", "mtf cl", tt, T.mnf[:], T.mtf[:], T.cl[:], A.min)
     op("v", "mxf", "mtf cl", tt, T.mxf[:], T.mtf[:], T.cl[:], A.max)
+    op("v", "uoff", "uoi", tc, T.uoff[:], T.uoi[:])
     op("v", "mnl", "mnf", tc, T.mnl[:], T.mnf[:])
     op("v", "mxl", "mxf", tc, T.mxl[:], T.mxf[:])
+    op("v", "uq", "ut", V.quantize_mx, T.uq[:, 0:128], T.uqs[:, 0:128], T.ut[:, 0:512])
+    op("v", "u2", "uq uoff", tc, T.u2[:, 0:128].bitcast(dt.uint32), T.uq[:, 0:128].bitcast(dt.uint32).indirect(T.uoff[:, 0:8]))
+    op("v", "u2s", "uq uoff", tc, T.u2s[:, 0:128], T.uqs[:, 0:128].indirect(T.uoff[:, 0:8]))
+    tolist(1)
     quantize_x(0)
     for b in range(4):
         op("v", "ec%d" % b, "wide", V.quantize_mx, T.ec[:, 128 * b:128 * b + 128], T.ecs[:, 128 * b:128 * b + 128], T.wide[:, 3 - b:515 - b])
 
-    def product(b, lhs, ls, a, rhs, rs, reads):
-        op("t", "b%d" % b, reads, P.matmul_mx, bank(b), lhs[:, a:a + 128], ls[:, a:a + 128], rhs[:, 0:C], rs[:, 0:C], True, True)
+    def product(b, lhs, ls, a, rhs, rs, reads, lo=0, hi=C):
+        op("t", "b%d" % b, reads, P.matmul_mx, bank(b, hi - lo), lhs[:, a:a + 128], ls[:, a:a + 128], rhs[:, lo:hi], rs[:, lo:hi], True, True)
 
     def plane(buf, b):
         return buf[:, C * b:C * b + C]
@@ -253,16 +256,17 @@ def rank_program(g, core, T, topo):
         send(nxt, T[lp % t][:, 0:C], xs[:, 0:C], "rx%d" % t)
         n = len(topo.engines(frm if came is None else came, core))
         wrote["land"], wrote["rl"] = ("rx%d" % t, 2 * n), ("rs%d" % t, n)
-        product(0, T.u2, T.u2s, 0, xq, xs, "u2 u2s xq%d" % t)
+        product(0, T.u2, T.u2s, 0, xq, xs, "u2 u2s xq%d" % t, 0, HALF)
+        product(7, T.u2, T.u2s, 0, xq, xs, "u2 u2s xq%d" % t, HALF, C)
         product(1, T.u2, T.u2s, 0, xq, xs, "u2 u2s xq%d" % t)
         for b in range(4):
             product(2 + b, T.ec, T.ecs, 128 * b, xq, xs, "ec%d xq%d" % (b, t))
         if t:
             tolist(1)
-        op("s", "sc", "b0", S.activation, T.sc[:], bank(0), COPY)
-        op("v", "sp", "b1 pen", tt, T.sp[:], bank(1), T.pen[:], A.min)
-        op("s", "n0", "sc jl0", S.activation, T.n0[:], ind(T.sc, jl(0)), COPY)
-        op("v", "m0", "sc jl0", tc, T.m0[:], ind(T.sc, jl(0)))
+        op("s", "sca", "b0", S.activation, T.sc[:, 0:HALF], bank(0, HALF), COPY)
+        op("v", "scb", "b7", tc, T.sc[:, HALF:C], bank(7, C - HALF))
+        op("s", "n0", "sca scb jl0", S.activation, T.n0[:], ind(T.sc, jl(0)), COPY)
+        op("v", "m0", "sca scb jl0", tc, T.m0[:], ind(T.sc, jl(0)))
         for k in range(6):
             m, m2, n1, n2 = "m%d" % k, "m%d" % (k + 1), "n%d" % (k % 2), "n%d" % ((k + 1) % 2)
             op("v", m2, "%s jl%d %s" % (m, k, n1), tt, T[m2][:], ind(T[m], jl(k)), T[n1][:], A.max)
@@ -272,6 +276,7 @@ def rank_program(g, core, T, topo):
                 tolist(k + 2)
         op("s", "m7", "m0 jl0", S.activation, T.m7[:], ind(T.m0, jl(0)), COPY)
         op("v", "cc", "m6 b1", tt, T.cc[:], T.m6[:], bank(1), A.is_le)
+        op("v", "sp", "b1 pen", tt, T.sp[:], bank(1), T.pen[:], A.min)
         op("v", "sm", "kb cc", scan, T.sm[:], T.kb[:], T.cc[:], 0.0, A.add, A.max)
         op("v", "el", "sm dsix", tt, T.el[:], lastm, T.dsix[:], A.mult)
         op("v", "posk", "csix el", tt, T.posk[:], T.csix[:], T.el[:], A.add)
@@ -319,37 +324,45 @@ def rank_program(g, core, T, topo):
         op("s", "jg0", "h0 mtl", S.activation, T.jg0[:], ind(T.h0, T.mtl[:, 0:L]), COPY)
         for b in range(4):
             op("s", "fz%d" % b, "b%d" % (2 + b), S.activation, plane(T.fz, b), bank(2 + b), COPY, scale=0.5)
-        op("v", "e1", "sc lstb", tc, T.e1[:], ind(T.sc, bl))
+        op("v", "e1", "sca scb lstb", tc, T.e1[:], ind(T.sc, bl))
         op("v", "e2", "e1 mxl", tc, T.e2[:], ind(T.e1, T.mxl[:, 0:L]))
         op("v", "cc", "e1 e2 mnl", tt, T.cc[:], ind(T.e1, T.mnl[:, 0:L]), T.e2[:], A.is_gt)
         keep("jg0")
         op("v", "fmf", "sj fk", tt, T.fmf[:], last, T.fk[:], A.subtract)
+        if t == 1:
+            op("v", "vq", "vt", V.quantize_mx, T.vq[:, 0:128], T.vqs[:, 0:128], T.vt[:, 0:512])
+        rl = T["rl%d" % t]
+        for lo, hi, b in ((0, 160, 0), (160, C, 0), (0, C, 1), (0, C, 2), (0, C, 3)):
+            op("s", "zp%d.%d" % (b, lo), "fz%d rl" % b, S.activation, T.zp[:, C * b + lo:C * b + hi],
+               ind(T.fz, rl[:, L + lo // 16:L + hi // 16], C * b), COPY)
+            op("v", "zt%d.%d" % (b, lo), "fz%d zp%d.%d rl" % (b, b, lo), tt, T.zt[:, 4 * lo + b:4 * hi:4],
+               ind(T.fz, rl[:, lo // 16:hi // 16], C * b), T.zp[:, C * b + lo:C * b + hi], A.add)
+        op("v", "zq", "zt0.0 zt0.160 zt1.0 zt2.0 zt3.0", V.quantize_mx, T.zq[:, 0:C], T.zqs[:, 0:C], T.zt[:, 0:B4])
+        hb = [6, 7, 2, 3]
+        product(6, T.wl, T.wls, 0, T.zq, T.zqs, "wl wls zq", 0, HALF)
+        product(4, T.wl, T.wls, 0, T.zq, T.zqs, "wl wls zq", HALF, C)
+        for b in range(1, 4):
+            product(hb[b], T.wl, T.wls, 128 * b, T.zq, T.zqs, "wl wls zq")
+        op("s", "hh0", "b6", S.activation, T.hh[:, 0:HALF], bank(6, HALF), COPY, scale=0.03125)
+        for b in range(1, 4):
+            op("s", "hh%d" % b, "b%d" % hb[b], S.activation, plane(T.hh, b), bank(hb[b]), COPY, scale=0.03125)
         op("v", "sm", "kb cc", scan, T.sm[:], T.kb[:], T.cc[:], 0.0, A.add, A.max)
         op("v", "bitl", "sm kb2", ts, T.bitl[:], lastm, kb2, None, A.subtract)
         op("v", "el", "bitl fmf", tt, T.el[:], T.bitl[:], T.fmf[:], A.mult)
-        op("v", "fk", "fk el", tt, T.fk[:], T.fk[:], T.el[:], A.add)
-        op("v", "jl0", "fk kj", ts, jl(0), T.fk[:], kj, None, A.subtract)
+        op("v", "hhb", "b4", ts, T.hh[:, HALF:C], bank(4, C - HALF), 0.03125, None, A.mult)
+        for b in range(4):
+            op("v", "xt%d" % b, "hh%d fo%d lstb" % (b, b) + (" hhb" if b == 0 else ""), tt, T.xt[:, b:B4:4],
+               ind(T.hh, bl, C * b), plane(T.fo, b), A.add)
+            if b == 0:
+                op("v", "fk", "fk el", tt, T.fk[:], T.fk[:], T.el[:], A.add)
+            if b == 1:
+                op("v", "jl0", "fk kj", ts, jl(0), T.fk[:], kj, None, A.subtract)
         hop0()
         if t < 2:
             hop(1)
         else:
             for i in range(8):
-                store("y", "h0", T.nf[i:i + 1, :], T.h0[16 * i:16 * i + 1, :])
-        rl = T["rl%d" % t]
-        for b in range(4):
-            op("s", "zp%d" % b, "fz%d rl" % b, S.activation, plane(T.zp, b), ind(T.fz, rl[:, L:2 * L], C * b), COPY)
-        for b in range(4):
-            op("v", "zt%d" % b, "fz%d zp%d rl" % (b, b), tt, T.zt[:, b:B4:4], ind(T.fz, rl[:, 0:L], C * b), plane(T.zp, b), A.add)
-        op("v", "zq", "zt0 zt1 zt2 zt3", V.quantize_mx, T.zq[:, 0:C], T.zqs[:, 0:C], T.zt[:, 0:B4])
-        hb = [6, 7, 2, 3]
-        for b in range(4):
-            product(hb[b], T.wl, T.wls, 128 * b, T.zq, T.zqs, "wl wls zq")
-        for b in range(4):
-            op("s", "hh%d" % b, "b%d" % hb[b], S.activation, plane(T.hh, b), bank(hb[b]), COPY, scale=0.03125)
-        for b in range(4):
-            op("v", "xt%d" % b, "hh%d fo%d lstb" % (b, b), tt, T.xt[:, b:B4:4], ind(T.hh, bl, C * b), plane(T.fo, b), A.add)
-        if t == 0:
-            op("v", "vq", "vt", V.quantize_mx, T.vq[:, 0:128], T.vqs[:, 0:128], T.vt[:, 0:512])
+                store("s", "h0", T.nf[i:i + 1, :], T.h0[16 * i:16 * i + 1, :])
     quantize_x(3)
     product(0, T.vq, T.vqs, 0, T.xq3, T.xs3, "vq xq3")
     store("y", "xq3", T.oc[:, 0:B4], T.xq3[:, 0:C].bitcast(dt.uint8))

@@ -205,38 +205,33 @@ def rank_program(g, core, T, topo):
         keep("h%d" % k)
         if k < 6:
             op("v", "jl%d" % k, "sj kj", ts, jl(k), last, kj, None, A.subtract)
-        else:
-            op("v", "dsix", "sj c0k", tt, T.dsix[:], last, T.c0k[:], A.subtract)
-            op("v", "dl", "dsix kb2", ts, T.dl[:], T.dsix[:], kb2, None, A.mult)
-            op("v", "csix", "c0k dl", tt, T.csix[:], T.c0k[:], T.dl[:], A.subtract)
+
 
     def quantize_x(t):
         src = "x0" if t == 0 else "xt"
         op("v", "xq%d" % t, "xt0 xt1 xt2 xt3" if t else "x0", V.quantize_mx,
            T["xq%d" % t][:, 0:C], T["xs%d" % t][:, 0:C], T[src][:, 0:B4])
 
+    FN = ActivationFunctionType
+    op("s", "rm", "j16", S.activation, T.rm[:], T.j16[:], FN.Sign)
+    op("s", "e1", "dd", S.activation, T.e1[:], T.dd[:], FN.Abs)
+    op("s", "e2", "e1", S.activation, T.e2[:], T.e1[:], FN.Relu, bias=1.0, scale=-1.0)
+    op("s", "pen", "e2", S.activation, T.pen[:], T.e2[:], FN.Identity, bias=-BIG, scale=2.0 * BIG)
     hop0()
     hop(1)
-    op("v", "e1", "dd", ts, T.e1[:], T.dd[:], 0.0, 2.0 * BIG, A.is_equal, A.mult)
-    op("v", "pen", "e1", ts, T.pen[:], T.e1[:], -BIG, None, A.add)
-    op("v", "rm", "j16", ts, T.rm[:], T.j16[:], 0.0, None, A.not_equal)
-    op("v", "cc", "dd", ts, T.cc[:], T.dd[:], 0.0, -8.0, A.is_equal, A.mult)
-    op("v", "cc2", "dd", ts, T.cc2[:], T.dd[:], 1.0, 2.0, A.is_equal, A.mult)
-    op("v", "kb", "cc cc2", tt, T.kb[:], T.cc[:], T.cc2[:], A.add)
+    op("v", "uoff", "uoi", tc, T.uoff[:], T.uoi[:])
+    op("v", "uq", "ut", V.quantize_mx, T.uq[:, 0:128], T.uqs[:, 0:128], T.ut[:, 0:512])
+    op("v", "u2", "uq uoff", tc, T.u2[:, 0:128].bitcast(dt.uint32), T.uq[:, 0:128].bitcast(dt.uint32).indirect(T.uoff[:, 0:8]))
+    op("s", "u2s", "uq uoff", S.activation, T.u2s[:, 0:128], T.uqs[:, 0:128].indirect(T.uoff[:, 0:8]), COPY)
+    op("s", "kb", "kk", S.activation, T.kb[:], T.kk[:], COPY, scale=2.0 / KB)
+    quantize_x(0)
+    tolist(1)
     op("v", "mtf", "mti", tc, T.mtf[:], T.mti[:])
     op("v", "mtl", "mti", tc, T.mtl[:], T.mti[:])
     op("v", "mnf", "mtf cl", tt, T.mnf[:], T.mtf[:], T.cl[:], A.min)
     op("v", "mxf", "mtf cl", tt, T.mxf[:], T.mtf[:], T.cl[:], A.max)
-    op("v", "uoff", "uoi", tc, T.uoff[:], T.uoi[:])
     op("v", "mnl", "mnf", tc, T.mnl[:], T.mnf[:])
     op("v", "mxl", "mxf", tc, T.mxl[:], T.mxf[:])
-    op("v", "uq", "ut", V.quantize_mx, T.uq[:, 0:128], T.uqs[:, 0:128], T.ut[:, 0:512])
-    op("v", "u2", "uq uoff", tc, T.u2[:, 0:128].bitcast(dt.uint32), T.uq[:, 0:128].bitcast(dt.uint32).indirect(T.uoff[:, 0:8]))
-    op("v", "u2s", "uq uoff", tc, T.u2s[:, 0:128], T.uqs[:, 0:128].indirect(T.uoff[:, 0:8]))
-    tolist(1)
-    quantize_x(0)
-    for b in range(4):
-        op("v", "ec%d" % b, "wide", V.quantize_mx, T.ec[:, 128 * b:128 * b + 128], T.ecs[:, 128 * b:128 * b + 128], T.wide[:, 3 - b:515 - b])
 
     def product(b, lhs, ls, a, rhs, rs, reads, lo=0, hi=C):
         op("t", "b%d" % b, reads, P.matmul_mx, bank(b, hi - lo), lhs[:, a:a + 128], ls[:, a:a + 128], rhs[:, lo:hi], rs[:, lo:hi], True, True)
@@ -259,8 +254,6 @@ def rank_program(g, core, T, topo):
         product(0, T.u2, T.u2s, 0, xq, xs, "u2 u2s xq%d" % t, 0, HALF)
         product(7, T.u2, T.u2s, 0, xq, xs, "u2 u2s xq%d" % t, HALF, C)
         product(1, T.u2, T.u2s, 0, xq, xs, "u2 u2s xq%d" % t)
-        for b in range(4):
-            product(2 + b, T.ec, T.ecs, 128 * b, xq, xs, "ec%d xq%d" % (b, t))
         if t:
             tolist(1)
         op("s", "sca", "b0", S.activation, T.sc[:, 0:HALF], bank(0, HALF), COPY)
@@ -274,9 +267,16 @@ def rank_program(g, core, T, topo):
                 hop(k + 2)
                 op("s", n2, m2, S.activation, T[n2][:], T[m2][:], COPY)
                 tolist(k + 2)
+            if k < 4:
+                if t == 0:
+                    op("v", "ec%d" % k, "wide", V.quantize_mx, T.ec[:, 128 * k:128 * k + 128], T.ecs[:, 128 * k:128 * k + 128], T.wide[:, 3 - k:515 - k])
+                product(2 + k, T.ec, T.ecs, 128 * k, xq, xs, "ec%d xq%d" % (k, t))
         op("s", "m7", "m0 jl0", S.activation, T.m7[:], ind(T.m0, jl(0)), COPY)
+        op("v", "dsix", "sj c0k", tt, T.dsix[:], last, T.c0k[:], A.subtract)
         op("v", "cc", "m6 b1", tt, T.cc[:], T.m6[:], bank(1), A.is_le)
+        op("v", "dl", "dsix kb2", ts, T.dl[:], T.dsix[:], kb2, None, A.mult)
         op("v", "sp", "b1 pen", tt, T.sp[:], bank(1), T.pen[:], A.min)
+        op("v", "csix", "c0k dl", tt, T.csix[:], T.c0k[:], T.dl[:], A.subtract)
         op("v", "sm", "kb cc", scan, T.sm[:], T.kb[:], T.cc[:], 0.0, A.add, A.max)
         op("v", "el", "sm dsix", tt, T.el[:], lastm, T.dsix[:], A.mult)
         op("v", "posk", "csix el", tt, T.posk[:], T.csix[:], T.el[:], A.add)
@@ -309,14 +309,15 @@ def rank_program(g, core, T, topo):
         op("v", "sk", "kk jg1", scan, T.sk[:], T.kk[:], T.jg1[:], 0.0, A.add, A.max)
         op("v", "dl", "sj posk", tt, T.dl[:], last, T.posk[:], A.subtract)
         op("v", "dl2", "sk c0k", tt, T.dl2[:], T.c0k[:], T.sk[:, 15:C:16], A.subtract)
+        op("v", "dl3", "sk sj", tt, T.dl3[:], T.sk[:, 15:C:16], last, A.subtract)
         op("v", "el", "sm dl", tt, T.el[:], lastm, T.dl[:], A.mult)
         op("v", "el2", "sm2 dl2", tt, T.el2[:], T.sm2[:, 15:C:16], T.dl2[:], A.mult)
-        op("v", "dl3", "sk sj", tt, T.dl3[:], T.sk[:, 15:C:16], last, A.subtract)
-        op("v", "posk", "posk el", tt, T.posk[:], T.posk[:], T.el[:], A.add)
-        op("v", "el2", "el2 dl3", tt, T.el2[:], T.el2[:], T.dl3[:], A.add)
+        op("v", "dl3", "dl3 sm", tt, T.dl3[:], T.dl3[:], lastm, A.mult)
         op("v", "el2", "el2 sm", tt, T.el2[:], T.el2[:], lastm, A.mult)
+        op("v", "posk", "posk el", tt, T.posk[:], T.posk[:], T.el[:], A.add)
+        op("v", "dl3", "dl3 sj", tt, T.dl3[:], T.dl3[:], last, A.add)
         op("v", "lstp", "posk kj", ts, lst[:, L:2 * L], T.posk[:], kj, None, A.subtract)
-        op("v", "el2", "el2 sj", tt, T.el2[:], T.el2[:], last, A.add)
+        op("v", "el2", "el2 dl3", tt, T.el2[:], T.el2[:], T.dl3[:], A.add)
         op("v", "lstb", "el2 kj", ts, lst[:, 0:L], T.el2[:], kj, None, A.subtract)
         before("g", ["lstb", "lstp"], [])
         send(nxt, T[ll % t][:, 0:2 * L], lst[:, 0:2 * L], "rs%d" % t)
@@ -364,12 +365,14 @@ def rank_program(g, core, T, topo):
             for i in range(8):
                 store("s", "h0", T.nf[i:i + 1, :], T.h0[16 * i:16 * i + 1, :])
     quantize_x(3)
-    product(0, T.vq, T.vqs, 0, T.xq3, T.xs3, "vq xq3")
+    product(0, T.vq, T.vqs, 0, T.xq3, T.xs3, "vq xq3", 0, HALF)
+    product(7, T.vq, T.vqs, 0, T.xq3, T.xs3, "vq xq3", HALF, C)
     store("y", "xq3", T.oc[:, 0:B4], T.xq3[:, 0:C].bitcast(dt.uint8))
-    op("v", "yo", "b0", tc, T.yo[:], bank(0))
+    op("s", "yoa", "b0", S.activation, T.yo[:, 0:HALF], bank(0, HALF), COPY)
+    op("v", "yob", "b7", tc, T.yo[:, HALF:C], bank(7, C - HALF))
     for k in range(4):
         store("s", "xq3", T.osc[4 * k:4 * k + 4, 0:C], T.xs3[32 * k:32 * k + 4, 0:C])
-    store("y", "yo", T.y[:], T.yo[:])
+    store("y", "yoa yob", T.y[:], T.yo[:])
     for q in ("v", "s", "t", "g"):
         wait("g", semname[q], cnt[q])
     wait("g", "ls", nsent[0])

from concourse.mybir import dt, AluOpType, ActivationFunctionType

C = 288
L = 18
B4 = 4 * C
HALF = C // 2
STEP = [4, 1, 2]
N = 8
BIG = 1e29
KB = 1024.0
F32, BF, I32, U16, F8, U8 = "float32", "bfloat16", "int32", "uint16", "float8_e4m3fn_x4", "uint8"


def _scratch():
    s = {}

    def sb(names, n, d):
        for k in names.split():
            s[k] = ("sbuf", [128, n], d)
    sb("pidx pi15", 1, I32)
    sb("icol kj kb2", 1, F32)
    sb("j16 dd kk pen idt sc sp jg0 jg1 sj e1 e2 sk yo n0 n1 m0 m1 m2 m3 m4 m5 m6 m7 h0 h1 h2 h3 h4 h5 h6", C, F32)
    sb("kb rm cc sm cc2 sm2", C, BF)
    sb("cl c0k posk dl el dl2 el2 dl3 bitl fk fmf dsix csix mtf mnf mxf", L, F32)
    sb("nxi mti", L, I32)
    sb("mnl mxl mtl jl0 jl1 jl2 jl3 jl4 jl5 pl0 pl1", L, U16)
    sb("lst0 lst1 lst2 rl0 rl1 rl2 rr0 rr1 rr2", 2 * L, U16)
    sb("uoi", 8, I32)
    sb("uoff", 8, U16)
    sb("ones wide", 516, BF)
    sb("ut vt", 512, BF)
    sb("x0 xt fo fz zp zt hh", B4, BF)
    for k, n in (("uq", 128), ("u2", 128), ("vq", 128), ("ec", 512), ("wl", 512), ("zq", C)):
        s[k] = ("sbuf", [128, n], F8)
        s[k + "s"] = ("sbuf", [128, n], U8)
    for t in range(4):
        s["xq%d" % t] = ("sbuf", [128, C], F8)
        s["xs%d" % t] = ("sbuf", [128, C], U8)
    for t in range(3):
        for a in "lr":
            s[a + "c%d" % t] = ("sbuf", [128, C], F8)
            s[a + "p%d" % t] = ("sbuf", [128, C], U8)
    s["ps"] = ("psum", [128, 4096], F32)
    return s


SCRATCH = _scratch()
SEMAPHORES = ["sv", "ss", "st", "sg", "ls", "out",
              "dx", "du", "dv", "dwc", "dws", "dn", "dm"] + [a + str(t) for t in range(3) for a in ("rx", "rs")]


def relay_of(topo, cores, a, b):
    if topo.may_write(a, b):
        return None
    for q in topo.cores_of(a):
        if q not in cores and topo.die(q) == topo.die(a) and topo.may_write(q, b):
            return q
    return None


def targets(topo, cores, core):
    out = []
    for d in STEP:
        for r in range(N):
            a, b = cores[r], cores[(r + d) % N]
            q = relay_of(topo, cores, a, b)
            if a == core:
                out.append(b if q is None else q)
            elif q == core:
                out.append(b)
    return out


def rank_program(g, core, T, topo):
    cores = list(T.cores)
    rank = T.rank_of(core)
    todo = targets(topo, cores, core)
    if not todo:
        return
    nsent = [0]

    def send(dst, out, src, sem):
        rid, pid = topo.addr(dst, core)
        g.remote_dma(out, src, T.sem[sem], T.sem.ls, pid, rid, topo.mask(core, dst))
        nsent[0] += len(topo.engines(core, dst))

    if rank is None:
        for t, d in enumerate(STEP):
            for r in range(N):
                a, b = cores[r], cores[(r + d) % N]
                if relay_of(topo, cores, a, b) != core:
                    continue
                n = len(topo.engines(a, core))
                g.wait_ge(T.sem["rx%d" % t], 2 * n)
                send(b, T["lc%d" % t][:, 0:C].bitcast(dt.uint8), T["rc%d" % t][:, 0:C].bitcast(dt.uint8), "rx%d" % t)
                send(b, T["lp%d" % t][:, 0:C], T["rp%d" % t][:, 0:C], "rx%d" % t)
                g.wait_ge(T.sem["rs%d" % t], n)
                send(b, T["rl%d" % t][:, 0:2 * L], T["rr%d" % t][:, 0:2 * L], "rs%d" % t)
        g.wait_ge(T.sem.ls, nsent[0])
        return

    A = AluOpType
    COPY = ActivationFunctionType.Copy
    queues = {"v": g.vector, "s": g.scalar, "t": g.tensor, "g": g, "y": g.sync}
    semname = {"v": "sv", "s": "ss", "t": "st", "g": "sg"}
    cnt = {"v": 0, "s": 0, "t": 0, "g": 0}
    seen, wrote, readers = {}, {}, {}

    def wait(q, sem, n):
        if seen.get((q, sem), 0) < n:
            queues[q].wait_ge(T.sem[sem], n)
            seen[(q, sem)] = n

    def before(q, reads, writes):
        need = {}
        for k in reads + writes:
            if k in wrote:
                s, n = wrote[k]
                need[s] = max(need.get(s, 0), n)
        for k in writes:
            for s, n in readers.get(k, {}).items():
                need[s] = max(need.get(s, 0), n)
        for s, n in need.items():
            wait(q, s, n)

    def op(q, writes, reads, fn, *args, **kw):
        writes, reads = writes.split(), reads.split()
        before(q, reads, writes)
        cnt[q] += 1
        fn(*args, **kw).then_inc(T.sem[semname[q]], 1)
        for k in reads:
            readers.setdefault(k, {})[semname[q]] = cnt[q]
        for k in writes:
            wrote[k] = (semname[q], cnt[q])
            readers[k] = {}

    V, S, P = g.vector, g.scalar, g.tensor
    ts, tt, tc, scan = V.tensor_scalar, V.tensor_tensor, V.tensor_copy, V.tensor_tensor_scan

    def load(q, name, out, src, sem):
        queues[q].dma_start(out, src).then_inc(T.sem[sem], 16)
        wrote[name] = (sem, 16)

    nout = [0]

    def store(q, reads, out, src):
        before(q, reads.split(), [])
        queues[q].dma_start(out, src).then_inc(T.sem.out, 16)
        nout[0] += 16

    def bank(b, n=C):
        return T.ps[:, 512 * b:512 * b + n]

    load("y", "x0", T.x0[:], T.x[:], "dx")
    load("s", "nxi", T.nxi[:], T.nx[:], "dn")
    load("s", "mti", T.mti[:], T.mt[:], "dm")
    load("s", "ut", T.ut[:], T.u[:], "du")
    wait("y", "dx", 16)
    wait("y", "du", 16)
    load("y", "wl", T.wl[:, 0:512].bitcast(dt.uint8), T.wc[:, 0:2048], "dwc")
    load("y", "wls", T.wls[:, 0:512], T.ws[:, 0:512], "dws")
    load("y", "vt", T.vt[:], T.v[:], "dv")

    op("g", "pidx", "", g.iota, T.pidx[:], [[0, 1]], 0, 1)
    op("g", "dl", "", g.iota, T.dl[:], [[16, L]], 0, 0, allow_small_or_imprecise_dtypes=True)
    op("g", "j16", "", g.iota, T.j16[:], [[0, L], [1, 16]], 0, 0, allow_small_or_imprecise_dtypes=True)
    op("g", "uoi", "", g.iota, T.uoi[:], [[16, 8]], 0, 0)
    op("g", "idt", "", g.iota, T.idt[:], [[1, C]], 0, 0, allow_small_or_imprecise_dtypes=True)
    op("v", "ones", "", V.memset, T.ones[:], 1.0)
    op("g", "wide", "ones", g.affine_select, T.wide[:], T.ones[:], [[-1, 516]], A.is_equal, 0.0, 3, 4)
    op("v", "pi15", "pidx", ts, T.pi15[:], T.pidx[:], 15, None, A.bitwise_and)
    op("v", "icol", "pi15", tc, T.icol[:], T.pi15[:])
    op("v", "kj", "icol", ts, T.kj[:], T.icol[:], 15.0, KB, A.is_lt, A.mult)
    op("v", "kb2", "icol", ts, T.kb2[:], T.icol[:], 15.0, 2.0, A.is_lt, A.mult)
    op("v", "cl", "dl icol", ts, T.cl[:], T.dl[:], T.icol[:, 0:1], None, A.add)
    op("v", "c0k", "cl kj", ts, T.c0k[:], T.cl[:], T.kj[:, 0:1], None, A.add)
    op("v", "dd", "j16 icol", ts, T.dd[:], T.j16[:], T.icol[:, 0:1], None, A.subtract)
    op("v", "m0", "dd", ts, T.m0[:], T.dd[:], 0.0, -4.0 * KB, A.is_equal, A.mult)
    op("v", "m1", "dd", ts, T.m1[:], T.dd[:], 1.0, KB, A.is_equal, A.mult)
    op("v", "kk", "m0 m1", tt, T.kk[:], T.m0[:], T.m1[:], A.add)
    op("v", "jl0", "nxi", tc, T.jl0[:], T.nxi[:])
    op("v", "dl2", "nxi", tc, T.dl2[:], T.nxi[:])
    kj, kb2 = T.kj[:, 0:1], T.kb2[:, 0:1]
    op("v", "fk", "dl2 kj", ts, T.fk[:], T.dl2[:], kj, None, A.add)

    last = T.sj[:, 15:C:16]
    lastm = T.sm[:, 15:C:16]

    def ind(buf, lst, a=0):
        return buf[:, a:a + C].indirect(lst)

    def jl(k):
        return T["jl%d" % k][:, 0:L]

    def keep(src):
        op("v", "sj", "kk " + src, scan, T.sj[:], T.kk[:], T[src][:], 0.0, A.add, A.max)

    def hop0():
        op("s", "h0", "idt jl0", S.activation, T.h0[:], ind(T.idt, jl(0)), COPY)

    def hop(k):
        op("s", "h%d" % k, "h%d jl%d" % (k - 1, k - 1), S.activation, T["h%d" % k][:], ind(T["h%d" % (k - 1)], jl(k - 1)), COPY)

    def tolist(k):
        keep("h%d" % k)
        if k < 6:
            op("v", "jl%d" % k, "sj kj", ts, jl(k), last, kj, None, A.subtract)


    def quantize_x(t):
        src = "x0" if t == 0 else "xt"
        op("v", "xq%d" % t, "xt0 xt1 xt2 xt3" if t else "x0", V.quantize_mx,
           T["xq%d" % t][:, 0:C], T["xs%d" % t][:, 0:C], T[src][:, 0:B4])

    FN = ActivationFunctionType
    op("s", "rm", "j16", S.activation, T.rm[:], T.j16[:], FN.Sign)
    op("s", "e1", "dd", S.activation, T.e1[:], T.dd[:], FN.Abs)
    op("s", "e2", "e1", S.activation, T.e2[:], T.e1[:], FN.Relu, bias=1.0, scale=-1.0)
    op("s", "pen", "e2", S.activation, T.pen[:], T.e2[:], FN.Identity, bias=-BIG, scale=2.0 * BIG)
    hop0()
    hop(1)
    op("v", "uoff", "uoi", tc, T.uoff[:], T.uoi[:])
    op("v", "uq", "ut", V.quantize_mx, T.uq[:, 0:128], T.uqs[:, 0:128], T.ut[:, 0:512])
    op("v", "u2", "uq uoff", tc, T.u2[:, 0:128].bitcast(dt.uint32), T.uq[:, 0:128].bitcast(dt.uint32).indirect(T.uoff[:, 0:8]))
    op("s", "u2s", "uq uoff", S.activation, T.u2s[:, 0:128], T.uqs[:, 0:128].indirect(T.uoff[:, 0:8]), COPY)
    op("s", "kb", "kk", S.activation, T.kb[:], T.kk[:], COPY, scale=2.0 / KB)
    quantize_x(0)
    tolist(1)
    op("v", "mtf", "mti", tc, T.mtf[:], T.mti[:])
    op("v", "mtl", "mti", tc, T.mtl[:], T.mti[:])
    op("v", "mnf", "mtf cl", tt, T.mnf[:], T.mtf[:], T.cl[:], A.min)
    op("v", "mxf", "mtf cl", tt, T.mxf[:], T.mtf[:], T.cl[:], A.max)
    op("v", "mnl", "mnf", tc, T.mnl[:], T.mnf[:])
    op("v", "mxl", "mxf", tc, T.mxl[:], T.mxf[:])

    def product(b, lhs, ls, a, rhs, rs, reads, lo=0, hi=C):
        op("t", "b%d" % b, reads, P.matmul_mx, bank(b, hi - lo), lhs[:, a:a + 128], ls[:, a:a + 128], rhs[:, lo:hi], rs[:, lo:hi], True, True)

    def plane(buf, b):
        return buf[:, C * b:C * b + C]

    for t, d in enumerate(STEP):
        to, frm = cores[(rank + d) % N], cores[(rank - d) % N]
        via, came = relay_of(topo, cores, core, to), relay_of(topo, cores, frm, core)
        xq, xs = T["xq%d" % t], T["xs%d" % t]
        if t:
            quantize_x(t)
        before("g", ["xq%d" % t], [])
        nxt, lc, lp, ll = (to, "lc%d", "lp%d", "rl%d") if via is None else (via, "rc%d", "rp%d", "rr%d")
        send(nxt, T[lc % t][:, 0:C].bitcast(dt.uint8), xq[:, 0:C].bitcast(dt.uint8), "rx%d" % t)
        send(nxt, T[lp % t][:, 0:C], xs[:, 0:C], "rx%d" % t)
        n = len(topo.engines(frm if came is None else came, core))
        wrote["land"], wrote["rl"] = ("rx%d" % t, 2 * n), ("rs%d" % t, n)
        product(0, T.u2, T.u2s, 0, xq, xs, "u2 u2s xq%d" % t, 0, HALF)
        product(7, T.u2, T.u2s, 0, xq, xs, "u2 u2s xq%d" % t, HALF, C)
        product(1, T.u2, T.u2s, 0, xq, xs, "u2 u2s xq%d" % t)
        if t:
            tolist(1)
        op("s", "sca", "b0", S.activation, T.sc[:, 0:HALF], bank(0, HALF), COPY)
        op("v", "scb", "b7", tc, T.sc[:, HALF:C], bank(7, C - HALF))
        op("s", "n0", "sca scb jl0", S.activation, T.n0[:], ind(T.sc, jl(0)), COPY)
        op("v", "m0", "sca scb jl0", tc, T.m0[:], ind(T.sc, jl(0)))
        for k in range(6):
            m, m2, n1, n2 = "m%d" % k, "m%d" % (k + 1), "n%d" % (k % 2), "n%d" % ((k + 1) % 2)
            op("v", m2, "%s jl%d %s" % (m, k, n1), tt, T[m2][:], ind(T[m], jl(k)), T[n1][:], A.max)
            if k < 5:
                hop(k + 2)
                op("s", n2, m2, S.activation, T[n2][:], T[m2][:], COPY)
                tolist(k + 2)
            if k < 4:
                if t == 0:
                    op("v", "ec%d" % k, "wide", V.quantize_mx, T.ec[:, 128 * k:128 * k + 128], T.ecs[:, 128 * k:128 * k + 128], T.wide[:, 3 - k:515 - k])
                product(2 + k, T.ec, T.ecs, 128 * k, xq, xs, "ec%d xq%d" % (k, t))
        op("s", "m7", "m0 jl0", S.activation, T.m7[:], ind(T.m0, jl(0)), COPY)
        op("v", "dsix", "sj c0k", tt, T.dsix[:], last, T.c0k[:], A.subtract)
        op("v", "cc", "m6 b1", tt, T.cc[:], T.m6[:], bank(1), A.is_le)
        op("v", "dl", "dsix kb2", ts, T.dl[:], T.dsix[:], kb2, None, A.mult)
        op("v", "sp", "b1 pen", tt, T.sp[:], bank(1), T.pen[:], A.min)
        op("v", "csix", "c0k dl", tt, T.csix[:], T.c0k[:], T.dl[:], A.subtract)
        op("v", "sm", "kb cc", scan, T.sm[:], T.kb[:], T.cc[:], 0.0, A.add, A.max)
        op("v", "el", "sm dsix", tt, T.el[:], lastm, T.dsix[:], A.mult)
        op("v", "posk", "csix el", tt, T.posk[:], T.csix[:], T.el[:], A.add)
        op("v", "pl0", "posk kj", ts, T.pl0[:], T.posk[:], kj, None, A.subtract)
        lst = T["lst%d" % t]
        at, key = T.pl0[:, 0:L], "pl0"
        for k in [5, 4, 3, 2, 1]:
            jg = "jg%d" % (k % 2)
            op("s", jg, "h%d %s" % (k, key), S.activation, T[jg][:], ind(T["h%d" % k], at), COPY)
            op("v", "cc", "m%d sp %s" % (k, key), tt, T.cc[:], ind(T["m%d" % k], at), T.sp[:], A.is_le)
            if k >= 2:
                b = 5 - k
                op("s", "fo%d" % b, "b%d" % (2 + b), S.activation, plane(T.fo, b), bank(2 + b), COPY)
                product(2 + b, T.ec, T.ecs, 128 * b, T["lc%d" % t], T["lp%d" % t], "land ec%d" % b)
            keep(jg)
            op("v", "sm", "rm cc", scan, T.sm[:], T.rm[:], T.cc[:], 0.0, A.mult, A.add)
            op("v", "dl", "sj posk", tt, T.dl[:], last, T.posk[:], A.subtract)
            op("v", "el", "sm dl", tt, T.el[:], lastm, T.dl[:], A.mult)
            op("v", "posk", "posk el", tt, T.posk[:], T.posk[:], T.el[:], A.add)
            key = "pl%d" % (k % 2)
            at = T[key][:, 0:L]
            op("v", key, "posk kj", ts, at, T.posk[:], kj, None, A.subtract)
        op("s", "jg0", "h0 " + key, S.activation, T.jg0[:], ind(T.h0, at), COPY)
        op("v", "cc", "m0 sp " + key, tt, T.cc[:], ind(T.m0, at), T.sp[:], A.is_le)
        op("s", "jg1", "h1 " + key, S.activation, T.jg1[:], ind(T.h1, at), COPY)
        op("v", "cc2", "m7 sp " + key, tt, T.cc2[:], ind(T.m7, at), T.sp[:], A.is_le)
        keep("jg0")
        op("v", "sm", "rm cc", scan, T.sm[:], T.rm[:], T.cc[:], 0.0, A.mult, A.add)
        op("v", "sm2", "rm cc2", scan, T.sm2[:], T.rm[:], T.cc2[:], 0.0, A.mult, A.add)
        op("v", "sk", "kk jg1", scan, T.sk[:], T.kk[:], T.jg1[:], 0.0, A.add, A.max)
        op("v", "dl", "sj posk", tt, T.dl[:], last, T.posk[:], A.subtract)
        op("v", "dl2", "sk c0k", tt, T.dl2[:], T.c0k[:], T.sk[:, 15:C:16], A.subtract)
        op("v", "dl3", "sk sj", tt, T.dl3[:], T.sk[:, 15:C:16], last, A.subtract)
        op("v", "el", "sm dl", tt, T.el[:], lastm, T.dl[:], A.mult)
        op("v", "el2", "sm2 dl2", tt, T.el2[:], T.sm2[:, 15:C:16], T.dl2[:], A.mult)
        op("v", "dl3", "dl3 sm", tt, T.dl3[:], T.dl3[:], lastm, A.mult)
        op("v", "el2", "el2 sm", tt, T.el2[:], T.el2[:], lastm, A.mult)
        op("v", "posk", "posk el", tt, T.posk[:], T.posk[:], T.el[:], A.add)
        op("v", "dl3", "dl3 sj", tt, T.dl3[:], T.dl3[:], last, A.add)
        op("v", "lstp", "posk kj", ts, lst[:, L:2 * L], T.posk[:], kj, None, A.subtract)
        op("v", "el2", "el2 dl3", tt, T.el2[:], T.el2[:], T.dl3[:], A.add)
        op("v", "lstb", "el2 kj", ts, lst[:, 0:L], T.el2[:], kj, None, A.subtract)
        before("g", ["lstb", "lstp"], [])
        send(nxt, T[ll % t][:, 0:2 * L], lst[:, 0:2 * L], "rs%d" % t)
        bl = lst[:, 0:L]
        op("s", "jg0", "h0 mtl", S.activation, T.jg0[:], ind(T.h0, T.mtl[:, 0:L]), COPY)
        for b in range(4):
            op("s", "fz%d" % b, "b%d" % (2 + b), S.activation, plane(T.fz, b), bank(2 + b), COPY, scale=0.5)
        op("v", "e1", "sca scb lstb", tc, T.e1[:], ind(T.sc, bl))
        op("v", "e2", "e1 mxl", tc, T.e2[:], ind(T.e1, T.mxl[:, 0:L]))
        op("v", "cc", "e1 e2 mnl", tt, T.cc[:], ind(T.e1, T.mnl[:, 0:L]), T.e2[:], A.is_gt)
        keep("jg0")
        op("v", "fmf", "sj fk", tt, T.fmf[:], last, T.fk[:], A.subtract)
        if t == 1:
            op("v", "vq", "vt", V.quantize_mx, T.vq[:, 0:128], T.vqs[:, 0:128], T.vt[:, 0:512])
        rl = T["rl%d" % t]
        for lo, hi, b in ((0, 160, 0), (160, C, 0), (0, C, 1), (0, C, 2), (0, C, 3)):
            op("s", "zp%d.%d" % (b, lo), "fz%d rl" % b, S.activation, T.zp[:, C * b + lo:C * b + hi],
               ind(T.fz, rl[:, L + lo // 16:L + hi // 16], C * b), COPY)
            op("v", "zt%d.%d" % (b, lo), "fz%d zp%d.%d rl" % (b, b, lo), tt, T.zt[:, 4 * lo + b:4 * hi:4],
               ind(T.fz, rl[:, lo // 16:hi // 16], C * b), T.zp[:, C * b + lo:C * b + hi], A.add)
        op("v", "zq", "zt0.0 zt0.160 zt1.0 zt2.0 zt3.0", V.quantize_mx, T.zq[:, 0:C], T.zqs[:, 0:C], T.zt[:, 0:B4])
        hb = [6, 7, 2, 3]
        product(6, T.wl, T.wls, 0, T.zq, T.zqs, "wl wls zq", 0, HALF)
        product(4, T.wl, T.wls, 0, T.zq, T.zqs, "wl wls zq", HALF, C)
        for b in range(1, 4):
            product(hb[b], T.wl, T.wls, 128 * b, T.zq, T.zqs, "wl wls zq")
        op("s", "hh0", "b6", S.activation, T.hh[:, 0:HALF], bank(6, HALF), COPY, scale=0.03125)
        for b in range(1, 4):
            op("s", "hh%d" % b, "b%d" % hb[b], S.activation, plane(T.hh, b), bank(hb[b]), COPY, scale=0.03125)
        op("v", "sm", "kb cc", scan, T.sm[:], T.kb[:], T.cc[:], 0.0, A.add, A.max)
        op("v", "bitl", "sm kb2", ts, T.bitl[:], lastm, kb2, None, A.subtract)
        op("v", "el", "bitl fmf", tt, T.el[:], T.bitl[:], T.fmf[:], A.mult)
        op("v", "hhb", "b4", ts, T.hh[:, HALF:C], bank(4, C - HALF), 0.03125, None, A.mult)
        for b in range(4):
            op("v", "xt%d" % b, "hh%d fo%d lstb" % (b, b) + (" hhb" if b == 0 else ""), tt, T.xt[:, b:B4:4],
               ind(T.hh, bl, C * b), plane(T.fo, b), A.add)
            if b == 0:
                op("v", "fk", "fk el", tt, T.fk[:], T.fk[:], T.el[:], A.add)
            if b == 1:
                op("v", "jl0", "fk kj", ts, jl(0), T.fk[:], kj, None, A.subtract)
        hop0()
        if t < 2:
            hop(1)
        else:
            for i in range(8):
                store("s", "h0", T.nf[i:i + 1, :], T.h0[16 * i:16 * i + 1, :])
    quantize_x(3)
    product(0, T.vq, T.vqs, 0, T.xq3, T.xs3, "vq xq3", 0, HALF)
    product(7, T.vq, T.vqs, 0, T.xq3, T.xs3, "vq xq3", HALF, C)
    store("y", "xq3", T.oc[:, 0:B4], T.xq3[:, 0:C].bitcast(dt.uint8))
    op("s", "yoa", "b0", S.activation, T.yo[:, 0:HALF], bank(0, HALF), COPY)
    op("v", "yob", "b7", tc, T.yo[:, HALF:C], bank(7, C - HALF))
    for k in range(4):
        store("s", "xq3", T.osc[4 * k:4 * k + 4, 0:C], T.xs3[32 * k:32 * k + 4, 0:C])
    store("y", "yoa yob", T.y[:], T.yo[:])
    for q in ("v", "s", "t", "g"):
        wait("g", semname[q], cnt[q])
    wait("g", "ls", nsent[0])
    wait("g", "out", nout[0])
